import numpy as np, ml_dtypes
CORES = [6,15,38,47]
N = 4
BF = ml_dtypes.bfloat16
def gentries(a):
    return np.ascontiguousarray(a.reshape(8, 16, -1).transpose(0, 2, 1)).reshape(8, -1)
def gtable(e):
    e = np.asarray(e); return np.ascontiguousarray(e.reshape(8, -1, 16).transpose(0, 2, 1)).reshape(128, -1).astype(np.int32)
V, W, D, RO = 1024, 4096, 16, 4
U = N * V
def family(rng):
    share = rng.permutation(np.array([1.0, 1.0, 1.0, 0.97, 0.95, 0.9, 0.6, 0.0])).reshape(8, 1, 1)
    q = rng.choice(np.array([2, 3, 4, 6]), (8, 16, 1)); often = rng.integers(0, 256, (8, 16, 8))
    v = np.take_along_axis(often, (rng.random((8, 16, W)) * q).astype(np.int64), 2)
    return np.where(rng.random((8, 16, W)) < share, v, rng.integers(0, 256, (8, 16, W)))
def parts(rng):
    return family(rng), rng.integers(0, 4096, (N, 8, V)), rng.integers(0, U, (N, 8, D, V))
def pack(f, c, e):
    return {"fam": np.ascontiguousarray(np.broadcast_to(f.reshape(1, 128, W), (N, 128, W))).astype(np.float32).astype(BF),
            "c0": np.stack([gtable(a) for a in c]), "nb": np.stack([gtable(a.reshape(8, -1)) for a in e])}
def setup_inputs(rng):
    return pack(*parts(rng))
def setup_inputs_ties(rng):
    f, c, e = parts(rng); f[:, 8:] = f[:, :8]; g = rng.permutation(8)
    f[g[0]] = rng.integers(0, 3, (1, W)); f[g[1]] = rng.integers(1, 256)
    return pack(f, c, e)
def setup_inputs_ends(rng):
    f, c, e = parts(rng); v = np.arange(V)[None, :]; a = int(rng.integers(0, N)); b = (a + 1) % N
    for r in range(N):
        e[r, 0] = rng.choice(np.array([0, U - 1, V - 1, V]), (D, V))
        e[r, 1] = np.where(rng.random((D, V)) < 0.5, r * V + v, e[r, 1]); e[r, 2] = e[r, 2, :1]
        e[r, 3] = ((r + 1) % N) * V + rng.integers(0, V, (D, V)); e[r, 4] = (r * V + v + 1 + np.arange(D)[:, None]) & (U - 1)
    e[:, 2] = b * V + (e[:, 2] & (V - 1)); e[:, 5] = b * V + int(rng.integers(0, V)); e[a] = b * V + (e[a] & (V - 1))
    c[:, 5:7] = rng.choice(np.array([0, 1, W - 1, 4094, 4095]), (N, 2, V))
    f[5] = 100 * rng.integers(0, 3, (16, W))
    f[6] = rng.integers(0, 256); f[6, 15] = np.where(rng.random(W) < 0.3, 255, rng.integers(0, 256, W))
    f[7] = rng.choice(np.array([0, 255]), (16, W)); c[:, :, 0] = 4095; c[:, :, V - 1] = 0
    c[:, 3] = (rng.permutation(U) & 4095).reshape(N, V); c[:, 4] = rng.integers(0, 4096)
    return pack(f, c, e)
def setup_inputs_same(rng):
    f, c, e = parts(rng); g = (int(rng.integers(0, 8)) + np.arange(8)) & 7
    c[:, g[0]] = rng.integers(0, 4096); c[:, g[1]] = rng.integers(0, 4096)
    c[:, g[2]] = rng.choice(rng.integers(0, 4096, 2), (N, V)); c[:, g[3]] = rng.integers(0, 4096, (N, 1))
    for i in (g[4], g[5]): f[i] = f[i][:, (np.arange(W) >> 3) << 3]
    return pack(f, c, e)
def setup_inputs_still(rng):
    f, c, e = parts(rng); c[:] = rng.integers(0, 4096, (1, 8, 1)); g = int(rng.integers(0, 8))
    for m in (g, (g + 4) & 7):
        h = (m + 7) & 7; one = int(c[0, m, 0]); two = one ^ (W >> 1); before = int(c[0, h, 0]); after = int(c[0, (m + 1) & 7, 0])
        o = rng.permutation(U); s = np.zeros(U, np.int64); s[o[U // 2:]] = 1
        e[:, m] = o[(e[:, m] & (U // 2 - 1)) + (U // 2) * s.reshape(N, 1, V)]
        c[:, m] = np.where(s == 1, two, one).reshape(N, V)
        f[h] = rng.integers(0, 256, (16, W)); f[m] = rng.integers(0, 256, (16, W))
        f[h, :, (before + two) & (W - 1)] = f[h, :, (before + one) & (W - 1)]
        f[m, 0, (two + after) & (W - 1)] = (int(f[m, 0, (one + after) & (W - 1)]) + int(rng.integers(1, 256))) & 255
    return pack(f, c, e)
def setup_inputs_spread(rng):
    ex = rng.permutation(np.array([1.0, 2.0, 4.0, 8.0, 20.0, 60.0, 200.0, 400.0])).reshape(8, 1, 1)
    f = (256 * rng.random((8, 16, W)) ** ex).astype(np.int64); up = rng.random((8, 16, 1)) < 0.5; f = np.where(up, 255 - f, f)
    c = (4096 * rng.random((N, 8, V)) ** rng.choice(np.array([1.0, 3.0, 6.0]), (N, 8, 1))).astype(np.int64)
    e = (U * rng.random((N, 8, D, V)) ** rng.choice(np.array([1.0, 2.0, 5.0]), (N, 8, D, 1))).astype(np.int64)
    return pack(f, c, e)
def check_inputs(d):
    bad = []
    for k, lo, hi in (("c0", 0, 4095), ("nb", 0, U - 1)):
        if np.min(d[k]) < lo or np.max(d[k]) > hi: bad.append("range of " + k)
    m = np.asarray(d["fam"]).astype(np.float32)
    if not np.all((m >= 0) & (m <= 255) & (m == np.floor(m))): bad.append("numbers of fam")
    if not np.all(m == m[:1]): bad.append("fam alike on all ranks")
    return bad
def reference(fam, c0, nb):
    f = fam.astype(np.float32).astype(np.int16).reshape(N, 8, 16, W)
    c = np.stack([gentries(a) for a in c0]).astype(np.int64)
    e = np.stack([gentries(a) for a in nb]).astype(np.int64).reshape(N, 8, D, V)
    k = np.arange(D)[:, None]
    for t in range(RO):
        ct = np.ascontiguousarray(c.transpose(1, 0, 2)).reshape(8, 1, U)
        look = (ct + np.roll(ct, -1, axis=0) + 1021 * t) & (W - 1)
        nc, ne, nx = [], [], []
        for a in range(N):
            p = np.take_along_axis(f[a], look, 2)
            own = p[:, :, a * V:(a + 1) * V]
            eq = np.take_along_axis(p, e[a].reshape(8, 1, D * V), 2).reshape(8, 16, D, V) == own[:, :, None, :]
            cnt = np.add.reduce(eq, axis=2, dtype=np.int64)
            x = np.argmin(cnt, axis=1)
            new = 256 * x + np.take_along_axis(own, x[:, None, :], 1)[:, 0].astype(np.int64)
            stay = np.take_along_axis(eq, x[:, None, None, :], 1)[:, 0]
            nc.append(new); nx.append(np.take_along_axis(cnt, x[:, None, :], 1)[:, 0])
            ne.append(np.where(stay, e[a], (37 * e[a] + 101 * new[:, None, :] + 811 * k + t) & (U - 1)))
        c = np.stack(nc); e = np.stack(ne); ex = np.stack(nx)
    return {"yc": np.stack([gtable(a) for a in c]).astype(np.float32), "yn": np.stack([gtable(a.reshape(8, -1)) for a in e]).astype(np.float32),
            "yx": np.stack([gtable(a) for a in ex]).astype(np.float32)}

@@ -1,0 +1,535 @@
+import math
+from concourse.bass import DstId, RemoteDMATransfer
+from concourse.mybir import AluOpType as Alu, ActivationFunctionType as Act
+
+N, V, U, D, RO = 4, 1024, 4096, 16, 4
+CH = [256, 256, 192, 192, 128]
+SHARE = [[5, 5, 4, 4, 0], [5, 5, 4, 3, 0], [5, 5, 4, 3, 0], [4, 5, 3, 4, 1]]
+LASTG = "VVV"
+NQB = 2
+NC = len(CH)
+BETA = 0.598
+BIG = 262144.0
+FW = 11264
+MATS = ["I", "I128", "nM", "M2", "I101", "I5", "DM", "ShI"] + ["Wd%d" % j for j in range(8)]
+SCALED = {"I128": 128.0, "nM": -BIG, "M2": 2 * BIG, "I101": 101.0, "I5": 5.0}
+for _j in range(8):
+    SCALED["Wd%d" % _j] = 2.0 ** (7 - _j)
+
+SCRATCH = {
+    "fam3": ("sbuf", [128, FW], "bfloat16"),
+    "pa0": ("sbuf", [128, U], "bfloat16"), "pa1": ("sbuf", [128, U], "bfloat16"),
+    "ow0": ("sbuf", [128, 2 * V], "bfloat16"), "ow1": ("sbuf", [128, 2 * V], "bfloat16"),
+    "eq": ("sbuf", [128, D * V], "bfloat16"), "gat": ("sbuf", [128, D * V], "bfloat16"),
+    "offs": ("sbuf", [128, 1024], "uint16"), "look": ("sbuf", [128, RO * N * 64], "uint16"),
+    "b": ("sbuf", [128, D, 64], "int32"), "w": ("sbuf", [128, D, 64], "int32"),
+    "u": ("sbuf", [128, D, 64], "float32"), "ynf": ("sbuf", [128, D, 64], "float32"),
+    "ca": ("sbuf", [128, 64], "int32"), "cb": ("sbuf", [128, 64], "int32"),
+    "cs": ("sbuf", [128, 64], "int32"), "ct": ("sbuf", [128, 64], "int32"),
+    "ci": ("sbuf", [128, 8], "int32"), "cf": ("sbuf", [128, 16], "float32"),
+    "colf": ("sbuf", [128, 144], "float32"), "colg": ("sbuf", [128, 128], "float32"),
+    "cm": ("sbuf", [128, 128 * len(MATS)], "bfloat16"), "tmpm": ("sbuf", [128, 144], "bfloat16"),
+    "tmpn": ("sbuf", [128, 128], "bfloat16"), "tmpo": ("sbuf", [128, 128], "bfloat16"),
+    "big": ("sbuf", [128, 144], "bfloat16"), "bigl": ("sbuf", [128, 144], "bfloat16"), "bigx": ("sbuf", [128, 144], "bfloat16"),
+    "kta": ("sbuf", [128, 1024], "bfloat16"), "ktb": ("sbuf", [128, 256], "bfloat16"),
+    "fla": ("sbuf", [128, 896], "bfloat16"), "flb": ("sbuf", [128, 256], "bfloat16"),
+    "pay": ("sbuf", [128, 5, 64], "bfloat16"), "ce": ("sbuf", [128, 256], "bfloat16"),
+    "ycf": ("sbuf", [128, 64], "float32"), "yxf": ("sbuf", [128, 64], "float32"),
+}
+for _s in "01":
+    SCRATCH["ww" + _s] = ("sbuf", [128, 256], "bfloat16")
+    SCRATCH["sg" + _s] = ("sbuf", [128, 256], "bfloat16")
+    SCRATCH["sel" + _s] = ("sbuf", [128, 5 * 256], "bfloat16")
+    for _n in ("AH", "C", "O", "Z"):
+        SCRATCH[_n + _s] = ("psum", [128, 512], "float32")
+
+SEMAPHORES = ["sV", "sS", "sP", "sG", "gi", "sent",
+              "d_ca", "d_cb", "d_cc", "d_fam", "d_nb", "d_f2", "d_f3", "d_yc", "d_yx", "d_y0", "d_y1", "d_y2", "d_y3"]
+SEMAPHORES += ["a0_0_%d" % r for r in range(N)]
+SEMAPHORES += ["a%d_%d_%d" % (t, c, r) for t in range(1, RO) for c in range(NC) for r in range(N)]
+SEMAPHORES += ["o%d_%d_%d" % (t, c, h) for t in range(1, RO) for c in range(NC) for h in range(2)]
+
+NOMINAL = {"cyc": 1.0, "pe": 0.5, "gam": 1.56, "lat": 110.0, "self": 60.0, "fix": 30.0, "issue": 900.0, "fly": 3000.0, "first": 2500.0,
+           "dlat": 2000.0, "dbw": 200.0}
+
+
+def R(name, a, b, step=1):
+    return (name, (slice(None), slice(a, b, step) if step != 1 else slice(a, b)), a, b)
+
+
+def R3(name, k0, k1, j0=0, j1=64):
+    return (name, (slice(None), slice(k0, k1), slice(j0, j1)), k0 * 64 + j0, (k1 - 1) * 64 + j1, j0, j1)
+
+
+def R1(name, k, j0=0, j1=64):
+    return (name, (slice(None), k, slice(j0, j1)), k * 64 + j0, k * 64 + j1, j0, j1)
+
+
+def meet(r, s):
+    return r[2] < s[3] and s[2] < r[3] and (len(r) < 6 or len(s) < 6 or (r[4] < s[5] and s[4] < r[5]))
+
+
+def M(name):
+    i = MATS.index(name)
+    return R("cm", 128 * i, 128 * i + 128)
+
+
+def wide(r):
+    return SCRATCH[r[0]][2] in ("float32", "int32")
+
+
+def in_psum(r):
+    return SCRATCH[r[0]][0] == "psum"
+
+
+def build(rank, ch, share):
+    ops = []
+    nc = len(ch)
+    full = slice(None)
+
+    def add(eng, call, cost, rd, wr, after=(), pad=0.0, sem=None):
+        ops.append({"eng": eng, "call": call, "cost": cost, "rd": list(rd), "wr": list(wr), "after": list(after), "pad": pad, "sem": sem})
+        return len(ops) - 1
+
+    def aps(*xs):
+        return [x for x in xs if isinstance(x, tuple)]
+
+    def ts(out, a, s1, s2, o0, o1, n, **k):
+        return add("V", ("ts", out, a, s1, s2, o0, o1), ("v", n * (1.0 if wide(out) or wide(a) else 0.5)), aps(a, s1, s2), [out], **k)
+
+    def tt(out, a, b, op, n, **k):
+        return add("V", ("tt", out, a, b, op), ("v", n * (1.0 if in_psum(a) or in_psum(b) else 2.0)), [a, b], [out], **k)
+
+    def cp(out, a, n, **k):
+        return add("V", ("cp", out, a), ("v", n * (1.0 if wide(out) or wide(a) else 0.5)), [a], [out], **k)
+
+    def act(out, a, f, bias, scale, n, **k):
+        return add("S", ("act", out, a, f, bias, scale), ("v", n), aps(a, bias, scale), [out], **k)
+
+    def mm(out, lhs, rhs, start, stop, n, **k):
+        return add("P", ("mm", out, lhs, rhs, start, stop), ("p", max(64, n)), [lhs, rhs], [out], **k)
+
+    def gather(eng, out, win, off, n, **k):
+        return add(eng, ("gv" if eng == "V" else "gs", out, win, off), ("g", n), [win, off], [out], **k)
+
+    def dma(q, sem, out, a, nbytes, rd, wr, **k):
+        return add(q, ("dma", out, a), ("d", nbytes), rd, wr, sem=sem, **k)
+
+    def lists(t, r, j0, j1):
+        return R("look", (t * N + r) * 64 + j0, (t * N + r) * 64 + j1)
+
+    def exchange(t, c, j0, j1):
+        s = add("G", ("send", lists(t, rank, j0, j1), "a%d_%d_%d" % (t, c, rank)), ("s", t == 0), [lists(t, rank, j0, j1)], [])
+        return s, [add("X", ("arr",), ("x", 0), [], [lists(t, r, j0, j1)], after=[s], sem="a%d_%d_%d" % (t, c, r)) for r in range(N) if r != rank]
+
+    def to_offsets(k0, k1, chunks):
+        for c in chunks:
+            v0, jn = sum(ch[:c]), ch[c] // 16
+            cp(R("offs", v0 + k0 * jn, v0 + k1 * jn), R3("b", k0, k1, v0 // 16, v0 // 16 + jn), (k1 - k0) * jn)
+
+    ranks = [rank] + [q for q in range(N) if q != rank]
+    dma("Y", "d_ca", ("ca", (full, full)), ("c0", (full, full)), 32768, [], [R("ca", 0, 64)])
+    dma("S", "d_cb", ("cb", (slice(0, 112), full)), ("c0", (slice(16, 128), full)), 28672, [], [R("cb", 0, 32)])
+    dma("S", "d_cc", ("cb", (slice(112, 128), full)), ("c0", (slice(0, 16), full)), 4096, [], [R("cb", 32, 64)])
+    dma("Y", "d_fam", ("fam3", (full, slice(0, U))), ("fam", (full, full)), 1 << 20, [], [R("fam3", 0, U)])
+    add("G", ("iota", R("ci", 0, 2), [[112, 2]], 1, False), ("i", 2), [], [R("ci", 0, 2)])
+    add("G", ("iota", R("colf", 0, 144), [[1, 144]], 0, True), ("i", 144), [], [R("colf", 0, 144)])
+    add("G", ("iota", R("colg", 0, 128), [[16, 8], [0, 16]], 0, True), ("i", 128), [], [R("colg", 0, 128)])
+    tt(R("cs", 0, 64), R("ca", 0, 64), R("cb", 0, 64), Alu.add, 64)
+    ts(R("ct", 0, 64), R("cs", 0, 64), U - 1, None, Alu.bitwise_and, None, 64)
+    cp(lists(0, rank, 0, 64), R("ct", 0, 64), 64)
+    s0, arr0 = exchange(0, 0, 0, 64)
+    dma("Y", "d_nb", ("b", (full, full, full)), ("nb", (full, full)), 1 << 19, [], [R("b", 0, 1024)], after=[s0])
+    ts(R("ci", 2, 4), R("ci", 0, 2), 112, None, Alu.bitwise_and, None, 2)
+    ts(R("ci", 4, 5), R("ci", 1, 2), 127, None, Alu.bitwise_and, None, 1)
+    ts(R("ci", 5, 6), R("ci", 0, 1), 15, None, Alu.bitwise_and, None, 1)
+    cp(R("cf", 0, 6), R("ci", 0, 6), 6)
+    ts(R("cf", 6, 8), R("cf", 2, 4), 15.0, None, Alu.add, None, 2)
+    ts(R("cf", 8, 9), R("cf", 5, 6), -BETA, 81.0, Alu.mult, Alu.add, 1)
+    ts(R("cf", 10, 11), R("cf", 5, 6), 128.0, None, Alu.mult, None, 1)
+    ts(R("cf", 11, 12), R("cf", 5, 6), 256.0, None, Alu.mult, None, 1)
+    ts(M("I"), R("colf", 0, 128), R("cf", 0, 1), None, Alu.is_equal, None, 128)
+    for name in SCALED:
+        act(M(name), M("I"), Act.Identity, 0.0, SCALED[name], 128)
+    ts(R("tmpn", 0, 128), R("colg", 0, 128), R("cf", 2, 3), -0.4, Alu.is_equal, Alu.mult, 128)
+    tt(M("DM"), R("tmpn", 0, 128), M("I"), Alu.add, 128)
+    ts(R("tmpo", 0, 128), R("colf", 0, 128), R("cf", 4, 5), None, Alu.is_equal, None, 128)
+    tt(M("ShI"), R("tmpo", 0, 128), M("I"), Alu.add, 128)
+    ts(R("big", 0, 144), R("colf", 0, 144), R("cf", 6, 7), None, Alu.is_equal, None, 144)
+    ts(R("tmpm", 0, 144), R("colf", 0, 144), R("cf", 7, 8), None, Alu.is_equal, None, 144)
+    tt(R("bigl", 0, 144), R("tmpm", 0, 144), R("big", 0, 144), Alu.add, 144)
+    ts(R("bigx", 0, 144), R("bigl", 0, 144), R("cf", 11, 12), None, Alu.mult, None, 144)
+    for kt, jw in (("kta", 64 - ch[-1] // 16), ("ktb", ch[-1] // 16)):
+        for k0, k1, val in ((0, 2, -129.0), (2, 14, 129.0), (14, 16, 258.0)):
+            add("V", ("ms", R(kt, k0 * jw, k1 * jw), val), ("v", (k1 - k0) * jw / 2), [], [R(kt, k0 * jw, k1 * jw)])
+    for r in ranks:
+        for h, eng in enumerate("VS"):
+            gather(eng, R("pa0", r * V + 512 * h, r * V + 512 * h + 512), R("fam3", 0, U), lists(0, r, 32 * h, 32 * h + 32), 512)
+    v0 = 0
+    for n in ch:
+        for h in range(2):
+            cp(R("ow0", 2 * v0 + h * n, 2 * v0 + h * n + n), R("pa0", rank * V + v0, rank * V + v0 + n), n)
+        v0 += n
+    to_offsets(0, D, range(nc))
+    dma("Y", "d_f2", ("fam3", (full, slice(U, 2 * U))), ("fam", (full, full)), 1 << 20, [], [R("fam3", U, 2 * U)], after=arr0)
+    dma("Y", "d_f3", ("fam3", (full, slice(2 * U, FW))), ("fam", (full, slice(0, FW - 2 * U))), 256 * (FW - 2 * U), [], [R("fam3", 2 * U, FW)], after=arr0)
+    win = R("fam3", 0, FW)
+
+    vlast, slast, count = [], [], 0
+    for t in range(RO):
+        final = t == RO - 1
+        ow, pn, on = "ow%d" % (t % 2), "pa%d" % ((t + 1) % 2), "ow%d" % ((t + 1) % 2)
+        pall = R("pa%d" % (t % 2), 0, U)
+        v0 = 0
+        for c, n in enumerate(ch):
+            z = str(count % 2)
+            count += 1
+            AH, C, O = "AH" + z, "C" + z, "O" + z
+            ww, sg, sel = "ww" + z, "sg" + z, "sel" + z
+            jn, j0, last, sh = n // 16, v0 // 16, c == nc - 1, share[t][c]
+            own2, own = R(ow, 2 * v0, 2 * v0 + 2 * n), R(ow, 2 * v0, 2 * v0 + n)
+            npay = 5 if final else 4
+
+            def pair(buf, j):
+                return R(buf, D * v0 + 2 * n * j, D * v0 + 2 * n * (j + 1))
+
+            def poff(j):
+                return R("offs", v0 + 2 * jn * j, v0 + 2 * jn * (j + 1))
+            if sh or last:
+                mm(R(O, 0, 2 * n), M("I"), own2, True, True, 2 * n)
+            for j in range(sh):
+                slast = [gather("S", pair("gat", j), pall, poff(j), 2 * n, after=slast)]
+            for i, j in enumerate(list(range(sh, 8)) + list(range(sh))):
+                if j >= sh:
+                    vlast = [add("V", ("ge", pair("eq", j), pall, poff(j), own2), ("g", 2 * n), [pall, poff(j), own2], [pair("eq", j)], after=vlast)]
+                else:
+                    vlast = [tt(pair("eq", j), pair("gat", j), R(O, 0, 2 * n), Alu.is_equal, 2 * n, after=vlast, pad=150.0)]
+                e0 = D * v0 + 2 * n * j
+                mm(R(C, 0, n), M("I"), R("eq", e0, e0 + n), i == 0, False, n)
+                mm(R(C, 0, n), M("I"), R("eq", e0 + n, e0 + 2 * n), False, i == 7, n)
+                mm(R(AH, 0, 2 * n), M("Wd%d" % j), pair("eq", j), i == 0, i == 7 and last, 2 * n)
+            lk = None if final else lists(t + 1, rank, j0, j0 + jn)
+            act(R(ww, 0, n), R(C, 0, n), Act.Exp, R("cf", 8, 9), -16 * BETA, n)
+            if last:
+                for k in range(D):
+                    ts(R1("u", k), R1("b", k), 37.0, float(811 * k + t), Alu.mult, Alu.add, 64, after=vlast)
+                mm(R("Z0", 0, n), M("DM"), R(ww, 0, n), True, True, n)
+                ts(R(sg, 0, n), R("Z0", 0, n), 0.0, None, Alu.is_gt, None, n)
+                tt(R(sel, 0, n), R(O, 0, n), R(sg, 0, n), Alu.mult, n)
+                if not final:
+                    for i in range(16):
+                        mm(R("Z1", 0, jn), R("bigx", 15 - i, 143 - i), R(sg, i, n, 16), i == 0, False, jn)
+                    for i in range(16):
+                        mm(R("Z1", 0, jn), R("bigl", 15 - i, 143 - i), R(sel, i, n, 16), False, i == 15, jn)
+                    ts(lk, R("Z1", 0, jn), float(1021 * (t + 1)), None, Alu.add, None, jn)
+                act(R(sel, n, 2 * n), R(sg, 0, n), Act.Identity, 0.0, R("cf", 11, 12), n)
+                for h in range(2):
+                    tt(R(sel, (2 + h) * n, (3 + h) * n), R(AH, h * n, h * n + n), R(sg, 0, n), Alu.mult, n)
+                if final:
+                    tt(R(sel, 4 * n, 5 * n), R(C, 0, n), R(sg, 0, n), Alu.mult, n)
+            else:
+                mm(R(O, 0, n), M("I"), own, True, False, n)
+                if final:
+                    act(R("ce", 0, n), R(C, 0, n), Act.Identity, 0.0, 1.0, n)
+                mm(R(C, 0, n), M("DM"), R(ww, 0, n), True, True, n)
+                act(R(sg, 0, n), R(C, 0, n), Act.Sign, 0.0, 1.0, n)
+                mm(R(O, 0, n), M("I128"), R(sg, 0, n), False, True, n)
+                mm(R(AH, 0, n), M("I128"), R(sg, 0, n), False, False, n)
+                mm(R(AH, n, 2 * n), M("I128"), R(sg, 0, n), False, True, n)
+                act(R(sel, n, 2 * n), R(sg, 0, n), Act.Identity, R("cf", 10, 11), R("cf", 10, 11), n)
+                act(R(sel, 0, n), R(O, 0, n), Act.Relu, -128.0, 1.0, n)
+                act(R(sel, 2 * n, 4 * n), R(AH, 0, 2 * n), Act.Relu, -128.0, 1.0, 2 * n)
+                if final:
+                    mm(R(C, 0, n), M("I"), R("ce", 0, n), True, False, n)
+                    mm(R(C, 0, n), M("I128"), R(sg, 0, n), False, True, n)
+                    act(R(sel, 4 * n, 5 * n), R(C, 0, n), Act.Relu, -128.0, 1.0, n)
+            for i in range(16):
+                mm(R(O, 0, npay * jn), R("big", 15 - i, 143 - i), R(sel, i, npay * n, 16), i == 0, i == 15, npay * jn)
+            act(R3("pay", 0, npay, j0, j0 + jn), R(O, 0, npay * jn), Act.Identity, 0.0, 1.0, npay * jn)
+            if not final:
+                if not last:
+                    for h in range(2):
+                        mm(R(C, 0, jn), M("ShI"), R1("pay", h, j0, j0 + jn), h == 0, h == 1, jn)
+                    ts(lk, R(C, 0, jn), float(1021 * (t + 1)), None, Alu.add, None, jn, pad=700.0)
+                arr = exchange(t + 1, c, j0, j0 + jn)[1]
+                for x, r in enumerate(ranks):
+                    gather(LASTG[x - 1] if last and x else "S", R(pn, r * V + v0, r * V + v0 + n), win, lists(t + 1, r, j0, j0 + jn), n,
+                           pad=0.0 if last or r == rank else 1500.0)
+                for h in range(2):
+                    o2, src = R(on, 2 * v0 + h * n, 2 * v0 + h * n + n), R(pn, rank * V + v0, rank * V + v0 + n)
+                    dma("Y", "o%d_%d_%d" % (t + 1, c, h), o2[:2], src[:2], 256 * n, [src], [o2], after=arr if c >= nc - 2 else [])
+            v0 += n
+        jl = 64 - ch[-1] // 16
+        zo = str(count % 2)
+        for ja, jb, banks in ((0, jl, ["AH" + zo, "O" + zo]), (jl, 64, ["Z0", "Z1"])):
+            jw = jb - ja
+            nq = 4 if ja == 0 else NQB
+            kq = D // nq
+            fl, kt = ("flb", "ktb") if ja else ("fla", "kta")
+            for j in range(7):
+                act(R(fl, 2 * j * jw, (2 * j + 2) * jw), R3("pay", 2, 4, ja, jb), Act.Identity, 128.502, 2.0 ** (j - 7), 2 * jw)
+            for q in range(nq):
+                Z, z0 = banks[q % 2], 256 * (q // 2)
+                k0, k1, wd = kq * q, kq * q + kq, kq * jw
+
+                def zs(a, b):
+                    return R(Z, z0 + jw * (a - k0), z0 + jw * (b - k0))
+                mm(zs(k0, k1), M("nM"), R(kt, jw * k0, jw * k1), True, False, wd)
+                mm(zs(k0, min(k1, 14)), M("nM"), R(fl, jw * k0, jw * min(k1, 14)), False, False, jw * (min(k1, 14) - k0))
+                mm(zs(max(k0, 2), k1), M("M2"), R(fl, jw * (max(k0, 2) - 2), jw * (k1 - 2)), False, False, jw * (k1 - max(k0, 2)))
+                for k in range(max(k0, 14), k1):
+                    mm(zs(k, k + 1), M("nM"), R1("pay", k - 12, ja, jb), False, False, jw)
+                for k in range(k0, k1):
+                    mm(zs(k, k + 1), M("I101"), R1("pay", 0, ja, jb), False, False, jw)
+                    mm(zs(k, k + 1), M("I5"), R1("pay", 1, ja, jb), False, k == k1 - 1, jw)
+                zq = zs(k0, k1)
+                tt(zq, zq, R3("u", k0, k1, ja, jb), Alu.add, wd, after=vlast)
+                tt(R3("w", k0, k1, ja, jb), zq, R3("b", k0, k1, ja, jb), Alu.max, wd)
+                ts(R3("b", k0, k1, ja, jb), R3("w", k0, k1, ja, jb), U - 1, None, Alu.bitwise_and, None, wd)
+                if final:
+                    cp(R3("ynf", k0, k1, ja, jb), R3("b", k0, k1, ja, jb), wd)
+                    if ja:
+                        for x in range(k0 // 4, k1 // 4):
+                            dma("Y", "d_y%d" % x, ("yn", (full, slice(256 * x, 256 * x + 256))), R3("ynf", 4 * x, 4 * x + 4)[:2], 1 << 17,
+                                [R3("ynf", 4 * x, 4 * x + 4)], [])
+                elif ja == 0 and q % 2:
+                    to_offsets(8 * (q // 2), 8 * (q // 2) + 8, range(nc - 1))
+            if ja and not final:
+                to_offsets(0, D, [nc - 1])
+        if final:
+            mm(R("C0", 0, 64), M("I"), R1("pay", 0), True, False, 64)
+            mm(R("C0", 0, 64), M("I"), R1("pay", 1), False, True, 64)
+            act(R("ycf", 0, 64), R("C0", 0, 64), Act.Identity, 0.0, 1.0, 64)
+            act(R("yxf", 0, 64), R1("pay", 4), Act.Identity, 0.0, 1.0, 64)
+            dma("S", "d_yc", ("yc", (full, full)), R("ycf", 0, 64)[:2], 32768, [R("ycf", 0, 64)], [])
+            dma("S", "d_yx", ("yx", (full, full)), R("yxf", 0, 64)[:2], 32768, [R("yxf", 0, 64)], [])
+    return ops
+
+
+def depend(ops):
+    hist, turns, deps = {}, {}, []
+    for i, o in enumerate(ops):
+        d = set()
+        acc = [(r, False) for r in o["rd"]] + [(r, True) for r in o["wr"]]
+        for r, wr in acc:
+            for (k, s, w2) in hist.get(r[0], []):
+                if (wr or w2) and meet(r, s):
+                    d.add(k)
+        for name in sorted(set(r[0] for r, wr in acc if in_psum(r))):
+            tn = turns.setdefault(name, [o["eng"], [], []])
+            if tn[0] != o["eng"]:
+                tn[:] = [o["eng"], [], tn[1]]
+            d.update(tn[2])
+            if o["eng"] == "P":
+                d.update(tn[1][-1:])
+            tn[1].append(i)
+        for r, wr in acc:
+            h = hist.setdefault(r[0], [])
+            if wr and len(r[1]) == 2 and r[1][1].step is None:
+                h[:] = [e for e in h if not (r[2] <= e[1][2] and e[1][3] <= r[3])]
+            h.append((i, r, wr))
+        deps.append(sorted(d))
+    return deps
+
+
+def times(o, P):
+    kind, n = o["cost"]
+    if kind == "v":
+        c = max(64, n) * P["cyc"] + P["fix"]
+    elif kind == "g":
+        c = n * P["gam"] * P["cyc"] + (50 if o["eng"] == "V" else 65)
+    elif kind == "p":
+        c = n * P["pe"]
+    elif kind == "i":
+        c = 130 + 2 * n * P["cyc"]
+    elif kind == "s":
+        c = P["issue"] + (P["first"] if n else 0)
+    elif kind == "x":
+        return 0.0, P["fly"]
+    else:
+        return 60.0 + (n / P["dbw"] if o["eng"] == "Y" else 0.0), P["dlat"] + n / P["dbw"]
+    return c, c
+
+
+def gap(ops, k, i, P):
+    a, b = ops[k]["eng"], ops[i]["eng"]
+    if b == "X" or (a == b == "P"):
+        return 0.0
+    return P["self"] if a == b and ops[k]["sem"] is None else P["lat"]
+
+
+def sweep(ops, tm, nxt, prio, back):
+    n = len(ops)
+    left, ready, start = [0] * n, [0.0] * n, [0.0] * n
+    for i in range(n):
+        for s, lag in nxt[i]:
+            left[s] += 1
+    cand = {e: [] for e in "VSPGYX"}
+    free = {e: 0.0 for e in "VSPGYX"}
+    for i in range(n):
+        if not left[i]:
+            cand[ops[i]["eng"]].append(i)
+    order = []
+    while len(order) < n:
+        best = None
+        for e in cand:
+            pick, limit = None, math.inf
+            for i in sorted(cand[e], key=lambda i: prio[i]):
+                st = max(ready[i] + (tm[i][1] - tm[i][0] if back else 0.0), free[e])
+                if pick is None or (st < pick[0] and st + tm[i][0] <= limit):
+                    pick = (st, i)
+                limit = min(limit, st + 120.0)
+            if pick is not None and (best is None or pick < best):
+                best = pick
+        st, i = best
+        e = ops[i]["eng"]
+        cand[e].remove(i)
+        free[e] = st + tm[i][0]
+        start[i] = st
+        order.append(i)
+        for s, lag in nxt[i]:
+            ready[s] = max(ready[s], st + (tm[i][0] if back or lag is None else tm[i][1]) + (lag or 0.0))
+            left[s] -= 1
+            if not left[s]:
+                cand[ops[s]["eng"]].append(s)
+    return order, start
+
+
+def schedule(ops, deps, P, passes=3):
+    n = len(ops)
+    succ, pred = [[] for _ in range(n)], [[] for _ in range(n)]
+    for i in range(n):
+        for k, hard in [(k, True) for k in deps[i]] + [(k, ops[k]["eng"] != ops[i]["eng"]) for k in ops[i]["after"]]:
+            lag = gap(ops, k, i, P) + ops[i]["pad"] if hard else None
+            succ[k].append((i, lag))
+            pred[i].append((k, lag))
+    tm = [times(o, P) for o in ops]
+    level = [0.0] * n
+    for i in range(n - 1, -1, -1):
+        level[i] = tm[i][1] + max([level[s] + (lag or 0.0) for s, lag in succ[i]] + [0.0])
+    order, start = sweep(ops, tm, succ, [-x for x in level], False)
+    best = (max(start[i] + tm[i][1] for i in range(n)), order)
+    for _ in range(passes):
+        back = sweep(ops, tm, pred, [-(start[i] + tm[i][1]) for i in range(n)], True)[1]
+        order, start = sweep(ops, tm, succ, [-(back[i] + tm[i][0]) for i in range(n)], False)
+        best = min(best, (max(start[i] + tm[i][1] for i in range(n)), order))
+    return best[1]
+
+
+def waits(ops, deps, order):
+    pos, cnt = {}, {}
+    for i in order:
+        cnt[ops[i]["eng"]] = cnt.get(ops[i]["eng"], 0) + 1
+        pos[i] = cnt[ops[i]["eng"]]
+    known = {e: {} for e in "VSPGY"}
+    seen, wl = {}, {}
+    for i in order:
+        e = ops[i]["eng"]
+        wl[i] = []
+        if e == "X":
+            seen[i] = {}
+            continue
+        kn = known[e]
+        need = set(deps[i]) | set(k for k in ops[i]["after"] if ops[k]["eng"] != e)
+        for k in sorted(need, key=lambda k: -pos[k]):
+            f = ops[k]["eng"]
+            if f == e == "P":
+                continue
+            key = ops[k]["sem"] or ("gi" if ops[k]["call"][0] == "send" else f)
+            if kn.get(key, 0) >= pos[k]:
+                continue
+            wl[i].append(k)
+            kn[key] = pos[k]
+            for a, v in seen[k].items():
+                kn[a] = max(kn.get(a, 0), v)
+        seen[i] = dict(kn)
+    return wl
+
+
+def rank_program(g, core, T, topo):
+    rank = T.rank_of(core)
+    if rank is None:
+        return
+    ops = build(rank, CH, SHARE)
+    deps = depend(ops)
+    order = schedule(ops, deps, NOMINAL)
+    wl = waits(ops, deps, order)
+    waited = set(k for i in order for k in wl[i])
+    queue = {"V": g.vector, "S": g.scalar, "P": g.tensor, "G": g, "Y": g.sync}
+    cores = list(T.cores)
+
+    def common(src):
+        m = -1
+        for d in cores:
+            if d != src:
+                m &= topo.mask(src, d)
+        return m
+
+    def hops(d):
+        a, b = topo.chip(core), topo.chip(d)
+        return 0 if a == b else 1 if topo.mates(a, b) or topo.same_plane(a, b) else 2
+    peers = sorted([d for d in cores if d != core], key=lambda d: -hops(d))
+    ids = [DstId(rid=topo.addr(d)[0], pnc=topo.addr(d)[1]) for d in peers]
+    mask = common(core)
+    width = {r: bin(common(cores[r])).count("1") for r in range(N)}
+
+    def ap(r):
+        return T[r[0]][r[1]] if isinstance(r, tuple) else r
+
+    signal, cnt, sends = {}, {}, 0
+    for i in order:
+        o = ops[i]
+        e, c = o["eng"], o["call"]
+        if e == "X":
+            signal[i] = (o["sem"], width[int(o["sem"][-1])])
+            continue
+        q = queue[e]
+        for k in wl[i]:
+            q.wait_ge(T.sem[signal[k][0]], signal[k][1])
+        kind = c[0]
+        if kind == "send":
+            g.remote_dma_fused([RemoteDMATransfer(dst_ids=ids, dma_engine_mask=mask, remote_sem=T.sem[c[2]], srcs=[ap(c[1])],
+                                                  dsts=[ap(c[1]) for _ in ids])], local_sem=T.sem["sent"])
+            sends += 1
+            if i in waited:
+                cnt["gi"] = cnt.get("gi", 0) + 1
+                g.sem_inc(T.sem["gi"], 1)
+                signal[i] = ("gi", cnt["gi"])
+            continue
+        if kind == "dma":
+            q.dma_start(ap(c[1]), ap(c[2])).then_inc(T.sem[o["sem"]], 16)
+            signal[i] = (o["sem"], 16)
+            continue
+        if kind == "ts":
+            if c[6] is None:
+                ins = q.tensor_scalar(ap(c[1]), ap(c[2]), ap(c[3]), None, c[5])
+            else:
+                ins = q.tensor_scalar(ap(c[1]), ap(c[2]), ap(c[3]), ap(c[4]), c[5], c[6])
+        elif kind == "tt":
+            ins = q.tensor_tensor(ap(c[1]), ap(c[2]), ap(c[3]), c[4])
+        elif kind == "cp":
+            ins = q.tensor_copy(ap(c[1]), ap(c[2]))
+        elif kind == "ms":
+            ins = q.memset(ap(c[1]), c[2])
+        elif kind == "act":
+            ins = q.activation(ap(c[1]), ap(c[2]), c[3], bias=ap(c[4]), scale=ap(c[5]))
+        elif kind == "mm":
+            ins = q.matmul(ap(c[1]), ap(c[2]), ap(c[3]), c[4], c[5])
+        elif kind == "gv":
+            ins = q.tensor_copy(ap(c[1]), ap(c[2]).indirect(ap(c[3])))
+        elif kind == "gs":
+            ins = q.activation(ap(c[1]), ap(c[2]).indirect(ap(c[3])), Act.Identity)
+        elif kind == "ge":
+            ins = q.tensor_tensor(ap(c[1]), ap(c[2]).indirect(ap(c[3])), ap(c[4]), Alu.is_equal)
+        elif c[4]:
+            ins = q.iota(ap(c[1]), c[2], 0, c[3], allow_small_or_imprecise_dtypes=True)
+        else:
+            ins = q.iota(ap(c[1]), c[2], 0, c[3])
+        if i in waited:
+            cnt[e] = cnt.get(e, 0) + 1
+            ins.then_inc(T.sem["s" + e], 1)
+            signal[i] = ("s" + e, cnt[e])
+    g.wait_ge(T.sem["sent"], sends * width[rank])
+    for i in order:
+        if ops[i]["sem"] is not None and i not in waited:
+            g.sync.wait_ge(T.sem[signal[i][0]], signal[i][1])

@@ -3,66 +3,93 @@ from concourse.bass import DstId, RemoteDMATransfer
 from concourse.mybir import AluOpType as Alu, ActivationFunctionType as Act
 
 N, V, U, D, RO = 4, 1024, 4096, 16, 4
-CH = [256, 256, 192, 192, 128]
-SHARE = [[5, 5, 4, 4, 0], [5, 5, 4, 3, 0], [5, 5, 4, 3, 0], [4, 5, 3, 4, 1]]
-LASTG = "VVV"
-NQB = 2
-NC = len(CH)
+CFG = {
+    "ch": [256, 128, 256, 256, 128],
+    "nd": [[0, 0, 8, 7, 0]] * 4,
+    "nq": [[0, 0, 0, 0, 0]] * 4,
+    "rp": 2,
+    "vm": [2, 2, 1, 1, 1],
+    "ride": [[0, 0, 1, 1, 0]] * 4,
+    "flv": 3, "qf": 1,
+    "merge": [[1, 1, 1, 0, 1]] * 4,
+    "ps": [0, 0, 0, 0, 0],
+    "pg": ["SSSS", "SSSS", "SSSS", "SVSS", "VSVV"],
+    "reg": [[[0, 1], [2, 3], [4]]] * 4,
+    "ob": [3, 0, 0, 1, 0], "lastb": [0, 1], "nef": 0,
+    "pad": 0.0, "dpad": 0.0, "alpha": 1.0, "urgent": ["sel4", "cnt4", "pg4"],
+    "pri": {'Ggs2': 6, 'Ggs3': 7, 'Gpg0': 15, 'Gpg1': 37, 'Gpg2': 6, 'Gpg3': 5, 'Gpg4': 16, 'Pah0': 30, 'Pah1': 88, 'Pah4': 31, 'Pcnt0': 22,
+            'Pcnt1': 15, 'Pcnt2': 14, 'Pcnt3': 18, 'Pcnt4': 29, 'Pne0': 34, 'Pne2': 67, 'Pne4': 14, 'Psel0': 9, 'Psel1': 13, 'Psel2': 17,
+            'Psel3': 2, 'Psel4': 52, 'Sgs2': 4, 'Sgs3': 17, 'Sne0': 17, 'Sne2': 2, 'Sne4': 23, 'Spg0': 19, 'Spg1': 16, 'Spg2': 95, 'Spg3': 18,
+            'Spg4': 5, 'Ssel0': 48, 'Ssel1': 23, 'Ssel2': -21, 'Ssel3': 7, 'Ssel4': 54, 'Vcmp2': 2, 'Vcmp3': -51, 'Vge0': 10, 'Vge1': 11,
+            'Vge3': 12, 'Vge4': 13, 'Vhalf': 69, 'Vne0': 55, 'Vne2': -51, 'Vne4': 49, 'Vpg3': 9, 'Vpg4': -52, 'Vsel0': 23, 'Vsel1': 1,
+            'Vsel2': -27, 'Vsel3': -30, 'Vsel4': 10},
+}
+CFG["pri"] = {'Ggs2':20,'Ggs3':17,'Gpg0':-16,'Gpg1':18,'Gpg2':3,'Gpg3':-25,'Gpg4':22,'Pah0':49,'Pah1':95,'Pah4':21,'Pcnt0':76,'Pcnt1':95,'Pcnt2':96,'Pcnt3':28,'Pcnt4':39,'Pne0':40,'Pne2':85,'Pne4':111,'Psel0':23,'Psel1':3,'Psel2':33,'Psel3':-15,'Psel4':45,'Sgs2':21,'Sgs3':28,'Sne0':19,'Sne2':26,'Sne4':21,'Spg0':89,'Spg1':25,'Spg2':60,'Spg3':23,'Spg4':24,'Ssel0':59,'Ssel1':1,'Ssel2':33,'Ssel3':13,'Ssel4':80,'Vcmp2':0,'Vcmp3':12,'Vge0':-19,'Vge1':11,'Vge3':11,'Vge4':18,'Vhalf':22,'Vne0':23,'Vne2':24,'Vne4':23,'Vpg3':-11,'Vpg4':10,'Vsel0':28,'Vsel1':2,'Vsel2':17,'Vsel3':-5,'Vsel4':0,'Pahl':54,'Pout':54,'Sahl':0,'Sout':21,'Vahl':22,'Yne4':-27,'Ypg0':12,'Ypg1':17,'Ypg2':-26,'Ypg3':12,'Ypg4':13,'Vhalf0':61,'Pah0F':107,'Pah1F':52,'Pah4F':83,'Pcnt0F':110,'Pcnt1F':109,'Pcnt2F':101,'Pcnt3F':92,'Pcnt4F':92,'Pne0F':131,'Pne2F':60,'Pne4F':98,'PoutF':116,'Psel0F':74,'Psel1F':105,'Psel2F':96,'Psel3F':66,'Psel4F':59,'Sgs2F':-1,'Sgs3F':97,'Sne0F':-55,'Sne2F':-43,'Sne4F':5,'SoutF':-52,'Ssel0F':68,'Ssel1F':96,'Ssel2F':98,'Ssel3F':10,'Ssel4F':69,'Vcmp2F':-62,'Vcmp3F':6,'Vge0F':-67,'Vge1F':-68,'Vge3F':-7,'Vge4F':-34,'VhalfF':-13,'Vne0F':-53,'Vne2F':-67,'Vne4F':-41,'Vsel2F':7,'Vsel3F':-93,'Vsel4F':36}
+CFG.update(reg=[[[0,1,2],[3,4]]]*4,pg=["SSSS","SSSS","SSSS","SSSS","VSVV"], pri={'Ggs2':-55,'Ggs3':-89,'Gpg0':-90,'Gpg1':-91,'Gpg2':-47,'Gpg3':-99,'Gpg4':-32,'Pah0':81,'Pah1':78,'Pah4':80,'Pcnt0':126,'Pcnt1':13,'Pcnt2':32,'Pcnt3':60,'Pcnt4':73,'Pne0':108,'Psel0':12,'Psel1':48,'Psel2':59,'Psel3':39,'Psel4':55,'Sgs2':12,'Sgs3':13,'Sne0':-6,'Spg0':65,'Spg1':64,'Spg2':13,'Spg3':82,'Spg4':83,'Ssel0':64,'Ssel1':64,'Ssel2':22,'Ssel3':-10,'Ssel4':-36,'Vcmp2':20,'Vcmp3':5,'Vge0':-6,'Vge1':-16,'Vge3':13,'Vge4':49,'Vhalf':78,'Vne0':37,'Vpg4':48,'Vsel0':-7,'Vsel1':30,'Vsel2':13,'Vsel3':10,'Vsel4':-11,'Pahl':79,'Sahl':16,'Sout':7,'Vahl':79,'Ypg0':-53,'Ypg1':-55,'Ypg2':-28,'Ypg3':-55,'Ypg4':-27,'Vhalf0':79,'Pah3':56,'Vah3':93,'Sah3':8,'Pne3':111,'Sne3':-7,'Vne3':49,'Vout':50,'Yne3':-16})
+CFG.update(sgs=[0] * 5, ch=[384,256,256,128],nd=[[0,8,7,0]]*4,nq=[[0]*4]*4,vm=[1,1,1,1],ride=[[0,1,1,0]]*4,merge=[[1,1,0,0]]*4,ps=[0]*4,pg=["SSSS","SSSS","SSSS","VSVV"],reg=[[[0,1],[2,3]]]*4,lastb=[3,0],urgent=["sel3","cnt3","pg3"])
+CFG["pri"] = {'Ggs1':-137,'Ggs2':-132,'Gpg0':-137,'Gpg1':-128,'Gpg2':-136,'Gpg3':-135,'Pah0':90,'Pah3':76,'Pcnt0':89,'Pcnt1':45,'Pcnt2':53,'Pcnt3':69,'Pne0':69,'Psel0':17,'Psel1':45,'Psel2':-2,'Psel3':67,'Sgs1':135,'Sgs2':151,'Sne0':129,'Spg0':231,'Spg1':139,'Spg2':141,'Spg3':153,'Ssel0':128,'Ssel1':147,'Ssel2':119,'Ssel3':146,'Vcmp1':44,'Vcmp2':-66,'Vge0':9,'Vge2':19,'Vge3':83,'Vhalf':-44,'Vne0':18,'Vpg3':-69,'Vsel0':-70,'Vsel1':-53,'Vsel2':-43,'Vsel3':15,'Pahl':39,'Sahl':150,'Sout':130,'Vahl':15,'Ypg0':21,'Ypg1':18,'Ypg2':-5,'Ypg3':2,'Vhalf0':-80,'Pah2':68,'Vah2':37,'Sah2':140,'Pne2':91,'Sne2':149,'Vne2':19,'Vout':-46,'Yne2':25,'Pah0F':31,'Pah3F':121,'Pcnt0F':130,'Pcnt1F':142,'Pcnt2F':120,'Pcnt3F':105,'Pne0F':129,'Pne2F':123,'Psel0F':129,'Psel1F':9,'Psel2F':49,'Psel3F':53,'Sgs1F':81,'Sgs2F':123,'Sne0F':122,'Sne2F':173,'SoutF':82,'Ssel0F':67,'Ssel1F':123,'Ssel2F':52,'Ssel3F':113,'Vcmp1F':33,'Vcmp2F':120,'Vge0F':15,'Vge2F':56,'Vge3F':147,'VhalfF':21,'Vne0F':44,'Vne2F':46,'VoutF':70,'Vsel1F':75,'Vsel2F':22,'Vsel3F':32}
 BETA = 0.598
-BIG = 262144.0
+BIG = 1048576.0
 FW = 11264
-MATS = ["I", "I128", "nM", "M2", "I101", "I5", "DM", "ShI"] + ["Wd%d" % j for j in range(8)]
-SCALED = {"I128": 128.0, "nM": -BIG, "M2": 2 * BIG, "I101": 101.0, "I5": 5.0}
+MATS = ["I", "I128", "nI", "nM", "M2", "Kp", "DM", "ShI"] + ["%s%d" % (a, j) for a in ("Wd", "Wr") for j in range(8)]
+MATS += ["K%d" % t for t in range(RO)]
+SCALED = {"I128": 128.0, "nI": -1.0, "nM": -BIG, "M2": 2 * BIG}
 for _j in range(8):
+    SCALED["Wr%d" % _j] = 1.0 - 2.0 ** (-1 - _j)
     SCALED["Wd%d" % _j] = 2.0 ** (7 - _j)
 
 SCRATCH = {
     "fam3": ("sbuf", [128, FW], "bfloat16"),
-    "pa0": ("sbuf", [128, U], "bfloat16"), "pa1": ("sbuf", [128, U], "bfloat16"),
-    "ow0": ("sbuf", [128, 2 * V], "bfloat16"), "ow1": ("sbuf", [128, 2 * V], "bfloat16"),
-    "eq": ("sbuf", [128, D * V], "bfloat16"), "gat": ("sbuf", [128, D * V], "bfloat16"),
+    "ow0": ("sbuf", [128, 8 * V], "bfloat16"), "ow1": ("sbuf", [128, 8 * V], "bfloat16"),
+    "eq": ("sbuf", [128, D * V], "bfloat16"),
     "offs": ("sbuf", [128, 1024], "uint16"), "look": ("sbuf", [128, RO * N * 64], "uint16"),
-    "b": ("sbuf", [128, D, 64], "int32"), "w": ("sbuf", [128, D, 64], "int32"),
-    "u": ("sbuf", [128, D, 64], "float32"), "ynf": ("sbuf", [128, D, 64], "float32"),
+    "bi": ("sbuf", [128, D, 64], "int32"), "w": ("sbuf", [128, D, 64], "int32"), "b16": ("sbuf", [128, D, 64], "float16"),
+    "b": ("sbuf", [128, D, 64], "float32"),
     "ca": ("sbuf", [128, 64], "int32"), "cb": ("sbuf", [128, 64], "int32"),
     "cs": ("sbuf", [128, 64], "int32"), "ct": ("sbuf", [128, 64], "int32"),
-    "ci": ("sbuf", [128, 8], "int32"), "cf": ("sbuf", [128, 16], "float32"),
+    "ci": ("sbuf", [128, 8], "int32"), "cf": ("sbuf", [128, 32], "float32"),
     "colf": ("sbuf", [128, 144], "float32"), "colg": ("sbuf", [128, 128], "float32"),
     "cm": ("sbuf", [128, 128 * len(MATS)], "bfloat16"), "tmpm": ("sbuf", [128, 144], "bfloat16"),
     "tmpn": ("sbuf", [128, 128], "bfloat16"), "tmpo": ("sbuf", [128, 128], "bfloat16"),
-    "big": ("sbuf", [128, 144], "bfloat16"), "bigl": ("sbuf", [128, 144], "bfloat16"), "bigx": ("sbuf", [128, 144], "bfloat16"),
-    "kta": ("sbuf", [128, 1024], "bfloat16"), "ktb": ("sbuf", [128, 256], "bfloat16"),
-    "fla": ("sbuf", [128, 896], "bfloat16"), "flb": ("sbuf", [128, 256], "bfloat16"),
-    "pay": ("sbuf", [128, 5, 64], "bfloat16"), "ce": ("sbuf", [128, 256], "bfloat16"),
+    "big": ("sbuf", [128, 144], "bfloat16"), "bigl": ("sbuf", [128, 144], "float16"),
+    "big16": ("sbuf", [128, 144], "float16"), "h37": ("sbuf", [128, 128], "float16"), "h101": ("sbuf", [128, 128], "float16"),
+    "shi16": ("sbuf", [128, 128], "float16"), "c16": ("sbuf", [128, 64], "float16"), "tmpf": ("sbuf", [128, 128], "float32"),
+    "kt": ("sbuf", [128, D, 64], "bfloat16"), "kc": ("sbuf", [128, D, 64], "bfloat16"), "fl": ("sbuf", [128, 14, 64], "bfloat16"),
+    "pay": ("sbuf", [128, 4, 64], "bfloat16"), "sel": ("sbuf", [128, 4, V], "bfloat16"), "sel16": ("sbuf", [128, 4, V], "float16"),
+    "cl": ("sbuf", [128, 2, 64], "bfloat16"), "fr": ("sbuf", [128, 2, 64], "float32"),
+    "cq": ("sbuf", [128, 2 * V], "bfloat16"), "sg": ("sbuf", [128, V], "bfloat16"), "ww": ("sbuf", [128, V], "bfloat16"),
     "ycf": ("sbuf", [128, 64], "float32"), "yxf": ("sbuf", [128, 64], "float32"),
 }
-for _s in "01":
-    SCRATCH["ww" + _s] = ("sbuf", [128, 256], "bfloat16")
-    SCRATCH["sg" + _s] = ("sbuf", [128, 256], "bfloat16")
-    SCRATCH["sel" + _s] = ("sbuf", [128, 5 * 256], "bfloat16")
-    for _n in ("AH", "C", "O", "Z"):
-        SCRATCH[_n + _s] = ("psum", [128, 512], "float32")
+for _t in range(RO):
+    SCRATCH["pa%d" % _t] = ("sbuf", [128, U], "bfloat16")
+    SCRATCH["Q%d" % _t] = ("psum", [128, 512], "float32")
+    SCRATCH["X%d" % _t] = ("psum", [128, 512], "float32")
 
 SEMAPHORES = ["sV", "sS", "sP", "sG", "gi", "sent",
               "d_ca", "d_cb", "d_cc", "d_fam", "d_nb", "d_f2", "d_f3", "d_yc", "d_yx", "d_y0", "d_y1", "d_y2", "d_y3"]
 SEMAPHORES += ["a0_0_%d" % r for r in range(N)]
-SEMAPHORES += ["a%d_%d_%d" % (t, c, r) for t in range(1, RO) for c in range(NC) for r in range(N)]
-SEMAPHORES += ["o%d_%d_%d" % (t, c, h) for t in range(1, RO) for c in range(NC) for h in range(2)]
+SEMAPHORES += ["a%d_%d_%d" % (t, c, r) for t in range(1, RO) for c in range(5) for r in range(N)]
+SEMAPHORES += ["o%d_%d" % (t, c) for t in range(RO) for c in range(5)]
+SEMAPHORES += ["g%d" % i for i in range(44)]
 
 NOMINAL = {"cyc": 1.0, "pe": 0.5, "gam": 1.56, "lat": 110.0, "self": 60.0, "fix": 30.0, "issue": 900.0, "fly": 3000.0, "first": 2500.0,
-           "dlat": 2000.0, "dbw": 200.0}
+           "dlat": 2000.0, "dbw": 260.0, "gissue": 1000.0, "rbw": 60.0}
 
 
 def R(name, a, b, step=1):
     return (name, (slice(None), slice(a, b, step) if step != 1 else slice(a, b)), a, b)
 
 
-def R3(name, k0, k1, j0=0, j1=64):
-    return (name, (slice(None), slice(k0, k1), slice(j0, j1)), k0 * 64 + j0, (k1 - 1) * 64 + j1, j0, j1)
+def R3(name, k0, k1, j0=0, j1=None, step=1):
+    w = SCRATCH[name][1][2]
+    j1 = w if j1 is None else j1
+    return (name, (slice(None), slice(k0, k1), slice(j0, j1, step) if step != 1 else slice(j0, j1)), k0 * w + j0, (k1 - 1) * w + j1, j0, j1)
 
 
-def R1(name, k, j0=0, j1=64):
-    return (name, (slice(None), k, slice(j0, j1)), k * 64 + j0, k * 64 + j1, j0, j1)
+def R1(name, k, j0=0, j1=None, step=1):
+    w = SCRATCH[name][1][2]
+    j1 = w if j1 is None else j1
+    return (name, (slice(None), k, slice(j0, j1, step) if step != 1 else slice(j0, j1)), k * w + j0, k * w + j1, j0, j1)
 
 
 def meet(r, s):
@@ -82,13 +109,21 @@ def in_psum(r):
     return SCRATCH[r[0]][0] == "psum"
 
 
-def build(rank, ch, share):
+def build(rank):
     ops = []
+    ch, rp = CFG["ch"], CFG["rp"]
     nc = len(ch)
+    at = [sum(ch[:c]) for c in range(nc + 1)]
     full = slice(None)
+    qb, nb = [], 0
+    for n in ch[:-1]:
+        qb.append(["Q%d" % nb, "Q%d" % (nb + (n > 256))])
+        nb += 1 + (n > 256)
+    ngd, tag = [0], ["", -1]
 
     def add(eng, call, cost, rd, wr, after=(), pad=0.0, sem=None):
-        ops.append({"eng": eng, "call": call, "cost": cost, "rd": list(rd), "wr": list(wr), "after": list(after), "pad": pad, "sem": sem})
+        ops.append({"eng": eng, "call": call, "cost": cost, "rd": list(rd), "wr": list(wr), "after": list(after), "pad": pad, "sem": sem,
+                    "tag": tag[0], "round": tag[1]})
         return len(ops) - 1
 
     def aps(*xs):
@@ -109,8 +144,8 @@ def build(rank, ch, share):
     def mm(out, lhs, rhs, start, stop, n, **k):
         return add("P", ("mm", out, lhs, rhs, start, stop), ("p", max(64, n)), [lhs, rhs], [out], **k)
 
-    def gather(eng, out, win, off, n, **k):
-        return add(eng, ("gv" if eng == "V" else "gs", out, win, off), ("g", n), [win, off], [out], **k)
+    def gather(eng, out, win, off, n, scale=1.0, **k):
+        return add(eng, ("gv" if eng == "V" else "gs", out, win, off, scale), ("g", n), [win, off], [out], **k)
 
     def dma(q, sem, out, a, nbytes, rd, wr, **k):
         return add(q, ("dma", out, a), ("d", nbytes), rd, wr, sem=sem, **k)
@@ -118,14 +153,28 @@ def build(rank, ch, share):
     def lists(t, r, j0, j1):
         return R("look", (t * N + r) * 64 + j0, (t * N + r) * 64 + j1)
 
-    def exchange(t, c, j0, j1):
-        s = add("G", ("send", lists(t, rank, j0, j1), "a%d_%d_%d" % (t, c, rank)), ("s", t == 0), [lists(t, rank, j0, j1)], [])
-        return s, [add("X", ("arr",), ("x", 0), [], [lists(t, r, j0, j1)], after=[s], sem="a%d_%d_%d" % (t, c, r)) for r in range(N) if r != rank]
+    def exchange(t, c, what, nbytes):
+        s = add("G", ("send", what(rank), "a%d_%d_%d" % (t, c, rank)), ("s", t == 0), [what(rank)], [])
+        return s, [add("X", ("arr",), ("x", nbytes), [], [what(r)], after=[s], sem="a%d_%d_%d" % (t, c, r)) for r in range(N) if r != rank]
 
-    def to_offsets(k0, k1, chunks):
-        for c in chunks:
-            v0, jn = sum(ch[:c]), ch[c] // 16
-            cp(R("offs", v0 + k0 * jn, v0 + k1 * jn), R3("b", k0, k1, v0 // 16, v0 // 16 + jn), (k1 - k0) * jn)
+    def to_offsets(k0, k1, c):
+        v0, jn = at[c], ch[c] // 16
+        off = R("offs", v0 + k0 * jn, v0 + k1 * jn)
+        cp(off, R3("bi", k0, k1, v0 // 16, v0 // 16 + jn), (k1 - k0) * jn)
+        was = list(tag)
+        tag[:] = ["half" if was[0] else "half0", tag[1] + 1]
+        ts(R3("b16", k0, k1, v0 // 16, v0 // 16 + jn), off, -2048.0, None, Alu.add, None, (k1 - k0) * jn)
+        tag[:] = was
+
+    def copies(t, c, **k):
+        n, v0 = ch[c], at[c]
+        src = R("pa%d" % t, rank * V + v0, rank * V + v0 + n)
+        for h in range(2 * max(min(rp, CFG["nd"][t][c]), CFG["vm"][c])):
+            o2 = R("ow%d" % (t % 2), 8 * v0 + h * n, 8 * v0 + h * n + n)
+            dma("Y", "o%d_%d" % (t, c), o2[:2], src[:2], 256 * n, [src], [o2], **k)
+
+    def cf(i):
+        return R("cf", i, i + 1)
 
     ranks = [rank] + [q for q in range(N) if q != rank]
     dma("Y", "d_ca", ("ca", (full, full)), ("c0", (full, full)), 32768, [], [R("ca", 0, 64)])
@@ -138,176 +187,282 @@ def build(rank, ch, share):
     tt(R("cs", 0, 64), R("ca", 0, 64), R("cb", 0, 64), Alu.add, 64)
     ts(R("ct", 0, 64), R("cs", 0, 64), U - 1, None, Alu.bitwise_and, None, 64)
     cp(lists(0, rank, 0, 64), R("ct", 0, 64), 64)
-    s0, arr0 = exchange(0, 0, 0, 64)
-    dma("Y", "d_nb", ("b", (full, full, full)), ("nb", (full, full)), 1 << 19, [], [R("b", 0, 1024)], after=[s0])
+    s0, arr0 = exchange(0, 0, lambda r: lists(0, r, 0, 64), 16384)
+    add("G", ("iota", R3("kc", 0, D), [[1, D], [0, 64]], 1, True), ("i", 1024), [], [R3("kc", 0, D)], after=[s0])
+    dma("S", "d_nb", ("bi", (full, full, full)), ("nb", (full, full)), 1 << 19, [], [R("bi", 0, 1024)])
     ts(R("ci", 2, 4), R("ci", 0, 2), 112, None, Alu.bitwise_and, None, 2)
     ts(R("ci", 4, 5), R("ci", 1, 2), 127, None, Alu.bitwise_and, None, 1)
     ts(R("ci", 5, 6), R("ci", 0, 1), 15, None, Alu.bitwise_and, None, 1)
     cp(R("cf", 0, 6), R("ci", 0, 6), 6)
     ts(R("cf", 6, 8), R("cf", 2, 4), 15.0, None, Alu.add, None, 2)
-    ts(R("cf", 8, 9), R("cf", 5, 6), -BETA, 81.0, Alu.mult, Alu.add, 1)
-    ts(R("cf", 10, 11), R("cf", 5, 6), 128.0, None, Alu.mult, None, 1)
-    ts(R("cf", 11, 12), R("cf", 5, 6), 256.0, None, Alu.mult, None, 1)
-    ts(M("I"), R("colf", 0, 128), R("cf", 0, 1), None, Alu.is_equal, None, 128)
+    ts(cf(8), cf(5), -BETA, 81.0, Alu.mult, Alu.add, 1)
+    ts(cf(9), cf(5), -BETA, 81.0 + 16 * BETA * 256, Alu.mult, Alu.add, 1)
+    ts(cf(10), cf(5), 128.0, None, Alu.mult, None, 1)
+    ts(cf(11), cf(5), 256.0, None, Alu.mult, None, 1)
+    ts(M("I"), R("colf", 0, 128), cf(0), None, Alu.is_equal, None, 128)
     for name in SCALED:
         act(M(name), M("I"), Act.Identity, 0.0, SCALED[name], 128)
-    ts(R("tmpn", 0, 128), R("colg", 0, 128), R("cf", 2, 3), -0.4, Alu.is_equal, Alu.mult, 128)
+    ts(R("h37", 0, 128), M("I"), 37.0, None, Alu.mult, None, 128)
+    ts(R("h101", 0, 128), M("I"), 101.0, None, Alu.mult, None, 128)
+    ts(R("tmpn", 0, 128), R("colg", 0, 128), cf(2), -0.4, Alu.is_equal, Alu.mult, 128)
     tt(M("DM"), R("tmpn", 0, 128), M("I"), Alu.add, 128)
-    ts(R("tmpo", 0, 128), R("colf", 0, 128), R("cf", 4, 5), None, Alu.is_equal, None, 128)
+    ts(R("tmpo", 0, 128), R("colf", 0, 128), cf(4), None, Alu.is_equal, None, 128)
     tt(M("ShI"), R("tmpo", 0, 128), M("I"), Alu.add, 128)
-    ts(R("big", 0, 144), R("colf", 0, 144), R("cf", 6, 7), None, Alu.is_equal, None, 144)
-    ts(R("tmpm", 0, 144), R("colf", 0, 144), R("cf", 7, 8), None, Alu.is_equal, None, 144)
+    cp(R("shi16", 0, 128), M("ShI"), 128)
+    ts(R("big", 0, 144), R("colf", 0, 144), cf(6), None, Alu.is_equal, None, 144)
+    ts(R("tmpm", 0, 144), R("colf", 0, 144), cf(7), None, Alu.is_equal, None, 144)
+    cp(R("big16", 0, 144), R("big", 0, 144), 144)
     tt(R("bigl", 0, 144), R("tmpm", 0, 144), R("big", 0, 144), Alu.add, 144)
-    ts(R("bigx", 0, 144), R("bigl", 0, 144), R("cf", 11, 12), None, Alu.mult, None, 144)
-    for kt, jw in (("kta", 64 - ch[-1] // 16), ("ktb", ch[-1] // 16)):
-        for k0, k1, val in ((0, 2, -129.0), (2, 14, 129.0), (14, 16, 258.0)):
-            add("V", ("ms", R(kt, k0 * jw, k1 * jw), val), ("v", (k1 - k0) * jw / 2), [], [R(kt, k0 * jw, k1 * jw)])
+    for k0, k1, val in ((0, 2, -129.0), (2, 14, 129.0), (14, 16, 258.0)):
+        add("V", ("ms", R3("kt", k0, k1), val), ("v", (k1 - k0) * 32), [], [R3("kt", k0, k1)])
+    ts(cf(12), cf(0), 0.0, 768.0, Alu.is_equal, Alu.mult, 1)
+    ts(cf(13), cf(0), 1.0, None, Alu.is_equal, None, 1)
+    ts(cf(14), cf(0), 2.0, None, Alu.is_equal, None, 1)
+    ts(cf(15), cf(13), 86.0, cf(12), Alu.mult, Alu.add, 1)
+    ts(cf(16), cf(14), -43.0, cf(15), Alu.mult, Alu.add, 1)
+    ts(cf(24), cf(0), 3.0, -70.0 * U, Alu.is_equal, Alu.mult, 1)
+    ts(cf(25), cf(0), 4.0, 70.0 * U, Alu.is_equal, Alu.mult, 1)
+    ts(cf(26), cf(16), cf(24), cf(25), Alu.add, Alu.add, 1)
+    ts(cf(17), cf(14), cf(13), None, Alu.subtract, None, 1)
+    for t in range(RO):
+        ts(cf(18 + t), cf(17), float(t), cf(26), Alu.mult, Alu.add, 1)
+        act(M("K%d" % t), M("I"), Act.Identity, cf(18 + t), 0.0, 128)
+    ts(cf(22), cf(0), 0.0, cf(13), Alu.is_equal, Alu.subtract, 1)
+    tt(R("tmpf", 0, 128), R("colg", 0, 128), R("colf", 0, 128), Alu.subtract, 128)
+    ts(R("tmpf", 0, 128), R("tmpf", 0, 128), 256.0, 2048.0, Alu.mult, Alu.add, 128)
+    ts(M("Kp"), R("tmpf", 0, 128), cf(22), None, Alu.mult, None, 128)
     for r in ranks:
         for h, eng in enumerate("VS"):
             gather(eng, R("pa0", r * V + 512 * h, r * V + 512 * h + 512), R("fam3", 0, U), lists(0, r, 32 * h, 32 * h + 32), 512)
-    v0 = 0
-    for n in ch:
-        for h in range(2):
-            cp(R("ow0", 2 * v0 + h * n, 2 * v0 + h * n + n), R("pa0", rank * V + v0, rank * V + v0 + n), n)
-        v0 += n
-    to_offsets(0, D, range(nc))
+    for c in range(nc):
+        copies(0, c)
+    for c in range(nc):
+        to_offsets(0, D, c)
     dma("Y", "d_f2", ("fam3", (full, slice(U, 2 * U))), ("fam", (full, full)), 1 << 20, [], [R("fam3", U, 2 * U)], after=arr0)
     dma("Y", "d_f3", ("fam3", (full, slice(2 * U, FW))), ("fam", (full, slice(0, FW - 2 * U))), 256 * (FW - 2 * U), [], [R("fam3", 2 * U, FW)], after=arr0)
     win = R("fam3", 0, FW)
 
-    vlast, slast, count = [], [], 0
     for t in range(RO):
         final = t == RO - 1
-        ow, pn, on = "ow%d" % (t % 2), "pa%d" % ((t + 1) % 2), "ow%d" % ((t + 1) % 2)
-        pall = R("pa%d" % (t % 2), 0, U)
-        v0 = 0
-        for c, n in enumerate(ch):
-            z = str(count % 2)
-            count += 1
-            AH, C, O = "AH" + z, "C" + z, "O" + z
-            ww, sg, sel = "ww" + z, "sg" + z, "sel" + z
-            jn, j0, last, sh = n // 16, v0 // 16, c == nc - 1, share[t][c]
-            own2, own = R(ow, 2 * v0, 2 * v0 + 2 * n), R(ow, 2 * v0, 2 * v0 + n)
-            npay = 5 if final else 4
+        tag[1] = t
+        ow, pn = "ow%d" % (t % 2), "pa%d" % (t + 1)
+        pall = R("pa%d" % t, 0, U)
 
-            def pair(buf, j):
-                return R(buf, D * v0 + 2 * n * j, D * v0 + 2 * n * (j + 1))
-
-            def poff(j):
-                return R("offs", v0 + 2 * jn * j, v0 + 2 * jn * (j + 1))
-            if sh or last:
-                mm(R(O, 0, 2 * n), M("I"), own2, True, True, 2 * n)
-            for j in range(sh):
-                slast = [gather("S", pair("gat", j), pall, poff(j), 2 * n, after=slast)]
-            for i, j in enumerate(list(range(sh, 8)) + list(range(sh))):
-                if j >= sh:
-                    vlast = [add("V", ("ge", pair("eq", j), pall, poff(j), own2), ("g", 2 * n), [pall, poff(j), own2], [pair("eq", j)], after=vlast)]
-                else:
-                    vlast = [tt(pair("eq", j), pair("gat", j), R(O, 0, 2 * n), Alu.is_equal, 2 * n, after=vlast, pad=150.0)]
-                e0 = D * v0 + 2 * n * j
-                mm(R(C, 0, n), M("I"), R("eq", e0, e0 + n), i == 0, False, n)
-                mm(R(C, 0, n), M("I"), R("eq", e0 + n, e0 + 2 * n), False, i == 7, n)
-                mm(R(AH, 0, 2 * n), M("Wd%d" % j), pair("eq", j), i == 0, i == 7 and last, 2 * n)
-            lk = None if final else lists(t + 1, rank, j0, j0 + jn)
-            act(R(ww, 0, n), R(C, 0, n), Act.Exp, R("cf", 8, 9), -16 * BETA, n)
-            if last:
-                for k in range(D):
-                    ts(R1("u", k), R1("b", k), 37.0, float(811 * k + t), Alu.mult, Alu.add, 64, after=vlast)
-                mm(R("Z0", 0, n), M("DM"), R(ww, 0, n), True, True, n)
-                ts(R(sg, 0, n), R("Z0", 0, n), 0.0, None, Alu.is_gt, None, n)
-                tt(R(sel, 0, n), R(O, 0, n), R(sg, 0, n), Alu.mult, n)
-                if not final:
-                    for i in range(16):
-                        mm(R("Z1", 0, jn), R("bigx", 15 - i, 143 - i), R(sg, i, n, 16), i == 0, False, jn)
-                    for i in range(16):
-                        mm(R("Z1", 0, jn), R("bigl", 15 - i, 143 - i), R(sel, i, n, 16), False, i == 15, jn)
-                    ts(lk, R("Z1", 0, jn), float(1021 * (t + 1)), None, Alu.add, None, jn)
-                act(R(sel, n, 2 * n), R(sg, 0, n), Act.Identity, 0.0, R("cf", 11, 12), n)
-                for h in range(2):
-                    tt(R(sel, (2 + h) * n, (3 + h) * n), R(AH, h * n, h * n + n), R(sg, 0, n), Alu.mult, n)
-                if final:
-                    tt(R(sel, 4 * n, 5 * n), R(C, 0, n), R(sg, 0, n), Alu.mult, n)
-            else:
-                mm(R(O, 0, n), M("I"), own, True, False, n)
-                if final:
-                    act(R("ce", 0, n), R(C, 0, n), Act.Identity, 0.0, 1.0, n)
-                mm(R(C, 0, n), M("DM"), R(ww, 0, n), True, True, n)
-                act(R(sg, 0, n), R(C, 0, n), Act.Sign, 0.0, 1.0, n)
-                mm(R(O, 0, n), M("I128"), R(sg, 0, n), False, True, n)
-                mm(R(AH, 0, n), M("I128"), R(sg, 0, n), False, False, n)
-                mm(R(AH, n, 2 * n), M("I128"), R(sg, 0, n), False, True, n)
-                act(R(sel, n, 2 * n), R(sg, 0, n), Act.Identity, R("cf", 10, 11), R("cf", 10, 11), n)
-                act(R(sel, 0, n), R(O, 0, n), Act.Relu, -128.0, 1.0, n)
-                act(R(sel, 2 * n, 4 * n), R(AH, 0, 2 * n), Act.Relu, -128.0, 1.0, 2 * n)
-                if final:
-                    mm(R(C, 0, n), M("I"), R("ce", 0, n), True, False, n)
-                    mm(R(C, 0, n), M("I128"), R(sg, 0, n), False, True, n)
-                    act(R(sel, 4 * n, 5 * n), R(C, 0, n), Act.Relu, -128.0, 1.0, n)
-            for i in range(16):
-                mm(R(O, 0, npay * jn), R("big", 15 - i, 143 - i), R(sel, i, npay * n, 16), i == 0, i == 15, npay * jn)
-            act(R3("pay", 0, npay, j0, j0 + jn), R(O, 0, npay * jn), Act.Identity, 0.0, 1.0, npay * jn)
-            if not final:
-                if not last:
-                    for h in range(2):
-                        mm(R(C, 0, jn), M("ShI"), R1("pay", h, j0, j0 + jn), h == 0, h == 1, jn)
-                    ts(lk, R(C, 0, jn), float(1021 * (t + 1)), None, Alu.add, None, jn, pad=700.0)
-                arr = exchange(t + 1, c, j0, j0 + jn)[1]
-                for x, r in enumerate(ranks):
-                    gather(LASTG[x - 1] if last and x else "S", R(pn, r * V + v0, r * V + v0 + n), win, lists(t + 1, r, j0, j0 + jn), n,
-                           pad=0.0 if last or r == rank else 1500.0)
-                for h in range(2):
-                    o2, src = R(on, 2 * v0 + h * n, 2 * v0 + h * n + n), R(pn, rank * V + v0, rank * V + v0 + n)
-                    dma("Y", "o%d_%d_%d" % (t + 1, c, h), o2[:2], src[:2], 256 * n, [src], [o2], after=arr if c >= nc - 2 else [])
-            v0 += n
-        jl = 64 - ch[-1] // 16
-        zo = str(count % 2)
-        for ja, jb, banks in ((0, jl, ["AH" + zo, "O" + zo]), (jl, 64, ["Z0", "Z1"])):
+        def new_ends(cs, banks):
+            ja, jb = at[cs[0]] // 16, at[cs[-1] + 1] // 16
             jw = jb - ja
-            nq = 4 if ja == 0 else NQB
-            kq = D // nq
-            fl, kt = ("flb", "ktb") if ja else ("fla", "kta")
+            tag[0] = "ne%d" % cs[0]
             for j in range(7):
-                act(R(fl, 2 * j * jw, (2 * j + 2) * jw), R3("pay", 2, 4, ja, jb), Act.Identity, 128.502, 2.0 ** (j - 7), 2 * jw)
-            for q in range(nq):
-                Z, z0 = banks[q % 2], 256 * (q // 2)
+                if final and jb == 64 and j < CFG["flv"]:
+                    ts(R3("fl", 2 * j, 2 * j + 2, ja, jb), R3("pay", 2, 4, ja, jb), 2.0 ** (j - 7), 128.502, Alu.mult, Alu.add, 2 * jw)
+                else:
+                    act(R3("fl", 2 * j, 2 * j + 2, ja, jb), R3("pay", 2, 4, ja, jb), Act.Identity, 128.502, 2.0 ** (j - 7), 2 * jw)
+            je = at[max([c + 1 for c in cs if c < nc - 1 and not CFG["ride"][t][c]] + [cs[0]])] // 16
+            if ja < je:
+                cw = R(banks[0], 448, 448 + je - ja)
+                for h in range(2):
+                    mm(cw, M("I"), R1("pay", h, ja, je), h == 0, h == 1, je - ja)
+                ts(R("c16", ja, je), cw, -2048.0, None, Alu.add, None, je - ja)
+            kq = D // len(banks)
+            for q, Z in enumerate(banks):
                 k0, k1, wd = kq * q, kq * q + kq, kq * jw
 
                 def zs(a, b):
-                    return R(Z, z0 + jw * (a - k0), z0 + jw * (b - k0))
-                mm(zs(k0, k1), M("nM"), R(kt, jw * k0, jw * k1), True, False, wd)
-                mm(zs(k0, min(k1, 14)), M("nM"), R(fl, jw * k0, jw * min(k1, 14)), False, False, jw * (min(k1, 14) - k0))
-                mm(zs(max(k0, 2), k1), M("M2"), R(fl, jw * (max(k0, 2) - 2), jw * (k1 - 2)), False, False, jw * (k1 - max(k0, 2)))
+                    return R(Z, jw * (a - k0), jw * (b - k0))
+                zq = zs(k0, k1)
+                bq, wq, iq = [R3(x, k0, k1, ja, jb) for x in ("b", "w", "bi")]
+                ka, kb = max(k0, 2), min(k1, 14)
+                mm(zq, M("nM"), R3("kt", k0, k1, ja, jb), True, False, wd)
+                mm(zs(k0, kb), M("nM"), R3("fl", k0, kb, ja, jb), False, False, jw * (kb - k0))
+                mm(zs(ka, k1), M("M2"), R3("fl", ka - 2, k1 - 2, ja, jb), False, False, jw * (k1 - ka))
                 for k in range(max(k0, 14), k1):
                     mm(zs(k, k + 1), M("nM"), R1("pay", k - 12, ja, jb), False, False, jw)
+                mm(zq, M("K%d" % t), R3("kc", k0, k1, ja, jb), False, False, wd)
                 for k in range(k0, k1):
-                    mm(zs(k, k + 1), M("I101"), R1("pay", 0, ja, jb), False, False, jw)
-                    mm(zs(k, k + 1), M("I5"), R1("pay", 1, ja, jb), False, k == k1 - 1, jw)
-                zq = zs(k0, k1)
-                tt(zq, zq, R3("u", k0, k1, ja, jb), Alu.add, wd, after=vlast)
-                tt(R3("w", k0, k1, ja, jb), zq, R3("b", k0, k1, ja, jb), Alu.max, wd)
-                ts(R3("b", k0, k1, ja, jb), R3("w", k0, k1, ja, jb), U - 1, None, Alu.bitwise_and, None, wd)
+                    mm(zs(k, k + 1), R("h101", 0, 128), R("c16", ja, jb), False, False, jw)
+                mm(zq, R("h37", 0, 128), R3("b16", k0, k1, ja, jb), False, True, wd)
+                tt(wq, zq, iq, Alu.max, wd)
+                ts(iq, wq, U - 1, None, Alu.bitwise_and, None, wd)
                 if final:
-                    cp(R3("ynf", k0, k1, ja, jb), R3("b", k0, k1, ja, jb), wd)
-                    if ja:
+                    cp(bq, iq, wd)
+                    if jb == 64:
                         for x in range(k0 // 4, k1 // 4):
-                            dma("Y", "d_y%d" % x, ("yn", (full, slice(256 * x, 256 * x + 256))), R3("ynf", 4 * x, 4 * x + 4)[:2], 1 << 17,
-                                [R3("ynf", 4 * x, 4 * x + 4)], [])
-                elif ja == 0 and q % 2:
-                    to_offsets(8 * (q // 2), 8 * (q // 2) + 8, range(nc - 1))
-            if ja and not final:
-                to_offsets(0, D, [nc - 1])
+                            dma("YS"[x % 2], "d_y%d" % x, ("yn", (full, slice(256 * x, 256 * x + 256))), R3("b", 4 * x, 4 * x + 4)[:2], 1 << 17,
+                                [R3("b", 4 * x, 4 * x + 4)], [])
+                elif k1 % 8 == 0 and cs[0] == 0:
+                    to_offsets(k1 - max(8, kq), k1, 0)
+            if final:
+                Z = banks[0]
+                for k in range(16):
+                    mm(R(Z, 448, 448 + jw), M("I" if k < 2 else "nI"), R1("pay", 2 + k, ja, jb) if k < 2 else R1("fl", k - 2, ja, jb), k == 0, k == 15, jw)
+                act(R("yxf", ja, jb), R(Z, 448, 448 + jw), Act.Identity, 14 * 129.0, 1.0, jw)
+            else:
+                for c in cs:
+                    if c:
+                        to_offsets(0, D, c)
+
+        for c, n in enumerate(ch):
+            v0 = at[c]
+            jn, j0, last, nd, nq, vm = n // 16, v0 // 16, c == nc - 1, CFG["nd"][t][c], CFG["nq"][t][c], CFG["vm"][c]
+            C, Q = ("X%d" % CFG["lastb"][0], "X%d" % CFG["lastb"][1]) if last else ("X%d" % c, qb[c][0])
+            ride, merge = CFG["ride"][t][c], final or (CFG["merge"][t][c] and not last)
+            O = Q if last else C
+            O2 = C if ride else "X%d" % CFG["ob"][c]
+            sel, big = ("sel16", "big16") if ride or last else ("sel", "big")
+            ww, sg = R("ww", v0, v0 + n), R("sg", v0, v0 + n)
+
+            def own(m):
+                return R(ow, 8 * v0, 8 * v0 + m * n)
+
+            def pair(j, m=1):
+                return R("eq", D * v0 + 2 * n * j, D * v0 + 2 * n * (j + m))
+
+            def poff(j, m=1):
+                return R("offs", v0 + 2 * jn * j, v0 + 2 * jn * (j + m))
+
+            def colours():
+                mm(R(O, 0, n), M("I"), own(1), True, False, n)
+                for a in range(0, n, 128):
+                    b = min(n, a + 128)
+                    mm(R(O, a, b), M("Kp"), R3("kc", 0, 2, 0, (b - a) // 2), False, b == n, b - a)
+
+            def ah(h):
+                return R(O, n + h * n, 2 * n + h * n) if last else R(qb[c][h], 0, n) if n > 256 else R(Q, h * n, h * n + n)
+            tag[0] = "cnt%d" % c
+            if last:
+                colours()
+            if nq:
+                mm(R(O2, 0, 2 * n), M("I"), own(2), True, True, 2 * n)
+            tag[0] = "gs%d" % c
+            for j in range(0, nd, rp):
+                m = min(rp, nd - j)
+                gather("S", pair(j, m), pall, poff(j, m), 2 * n * m, -1.0)
+                add("G", ("gd", pair(j, m), own(2 * m)), ("gd", 512 * n * m, ngd[0] == 0), [own(2 * m), pair(j, m)], [pair(j, m)], sem="g%d" % ngd[0])
+                ngd[0] += 1
+            for j in range(nd, nd + nq):
+                gather("S", pair(j), pall, poff(j), 2 * n)
+            late = max(0, nd - CFG["qf"] * rp) // rp * rp
+            for i, j in enumerate(list(range(nd + nq, 8)) + list(range(late)) + list(range(nd, nd + nq)) + list(range(late, nd))):
+                tag[0] = ("ge%d" if j >= nd + nq else "cmp%d") % c
+                if j >= nd + nq:
+                    if (7 - j) % vm == vm - 1 or j == nd + nq:
+                        m = (7 - j) % vm + 1
+                        add("V", ("ge", pair(j, m), pall, poff(j, m), own(2 * m)), ("g", 2 * n * m), [pall, poff(j, m), own(2 * m)], [pair(j, m)])
+                elif j >= nd:
+                    tt(pair(j), pair(j), R(O2, 0, 2 * n), Alu.is_equal, 2 * n, pad=150.0)
+                elif j % rp == 0:
+                    m = min(rp, nd - j)
+                    ts(pair(j, m), pair(j, m), 0.0, None, Alu.is_equal, None, 2 * n * m, pad=CFG["dpad"])
+                e0 = D * v0 + 2 * n * j
+                tag[0] = "cnt%d" % c
+                if ride:
+                    mm(R(Q, 0, 2 * n), M("Wr%d" % j), pair(j), i == 0, i == 7, 2 * n)
+                else:
+                    mm(R(C, 0, n), M("I"), R("eq", e0, e0 + n), i == 0, False, n)
+                    mm(R(C, 0, n), M("I"), R("eq", e0 + n, e0 + 2 * n), False, i == 7, n)
+                    tag[0] = "ah%d" % c
+                    if n > 256:
+                        for h in range(2):
+                            mm(ah(h), M("Wd%d" % j), R("eq", e0 + h * n, e0 + h * n + n), i == 0, False, n)
+                    else:
+                        mm(R(O, n, 3 * n) if last else R(Q, 0, 2 * n), M("Wd%d" % j), pair(j), i == 0, last and i == 7, 2 * n)
+            tag[0] = "sel%d" % c
+            lk = None if final else lists(t + 1, rank, j0, j0 + jn)
+            cw = R(C, 256, 256 + n) if ride else R(C, 0, n)
+            if ride:
+                cq = R("cq", 2 * v0, 2 * v0 + 2 * n)
+                colours()
+                act(cq, R(Q, 0, 2 * n), Act.Identity, 128.498, 1.0, 2 * n)
+                for h in range(2):
+                    mm(cw, M("I"), R("cq", 2 * v0 + h * n, 2 * v0 + h * n + n), h == 0, h == 1, n)
+            if last or ride:
+                act(ww, cw, Act.Exp, cf(9 if ride else 8), -16 * BETA, n)
+                mm(cw, M("DM"), ww, True, True, n)
+                if CFG["sgs"][c]:
+                    act(ww, cw, Act.Sign, 0.0, 1.0, n)
+                    act(sg, ww, Act.Identity, 0.5, 0.5, n)
+                else:
+                    ts(sg, cw, 0.0, None, Alu.is_gt, None, n)
+                tt(R1(sel, 1, v0, v0 + n), R(O, 0, n), sg, Alu.mult, n)
+            else:
+                act(ww, R(C, 0, n), Act.Exp, cf(8), -16 * BETA, n)
+                mm(R(C, 0, n), M("DM"), ww, True, True, n)
+                act(sg, R(C, 0, n), Act.Sign, 0.0, 1.0, n)
+                mm(R(O, 0, n), M("I"), own(1), True, False, n)
+                mm(R(O, 0, n), M("I128"), sg, False, True, n)
+                act(R1("sel", 1, v0, v0 + n), sg, Act.Identity, cf(10), cf(10), n)
+                act(R1("sel", 0, v0, v0 + n), R(O, 0, n), Act.Relu, -128.0, 1.0, n)
+
+            def bytes_of_winner():
+                for h in range(2):
+                    if ride or last:
+                        tt(R1(sel, 2 + h, v0, v0 + n), ah(h), sg, Alu.mult, n)
+                    else:
+                        mm(ah(h), M("I128"), sg, False, h == 1 or n > 256, n)
+                        if n > 256:
+                            act(R1(sel, 2 + h, v0, v0 + n), ah(h), Act.Relu, -128.0, 1.0, n)
+                if not (ride or last or n > 256):
+                    act(R3(sel, 2, 4, v0, v0 + n), R(Q, 0, 2 * n), Act.Relu, -128.0, 1.0, 2 * n)
+
+            def to_lists(bank, a, b):
+                for i in range(16):
+                    mm(R(bank, 0, (b - a) * jn), R(big, 15 - i, 143 - i), R3(sel, a, b, v0 + i, v0 + n, 16), i == 0, i == 15, (b - a) * jn)
+                if not (last or ride):
+                    act(R3("pay", a, b, j0, j0 + jn), R(bank, 0, (b - a) * jn), Act.Identity, 0.0, 1.0, (b - a) * jn)
+                    return
+                cp(R("c16", j0, j0 + jn), R(bank, 0, jn), jn)
+                qs, cl, fr = R(bank, jn, 3 * jn), R3("cl", 0, 2, j0, j0 + jn), R3("fr", 0, 2, j0, j0 + jn)
+                if last:
+                    act(R3("pay", 2, 4, j0, j0 + jn), qs, Act.Identity, 0.0, 1.0, 2 * jn)
+                else:
+                    act(cl, qs, Act.Identity, 128.498, 1.0, 2 * jn)
+                    tt(fr, qs, cl, Alu.subtract, 2 * jn)
+                    act(R3("pay", 2, 4, j0, j0 + jn), fr, Act.Identity, -32768.0, -256.0, 2 * jn)
+            if merge:
+                bytes_of_winner()
+            if merge or not (last or ride):
+                to_lists(O, 1 if last or ride else 0, 4 if merge else 2)
+            if not final:
+                lw = R(C, 448, 448 + jn)
+                if not (last or ride):
+                    for h in range(2):
+                        mm(lw, M("ShI"), R1("pay", h, j0, j0 + jn), h == 0, h == 1, jn)
+                elif merge:
+                    mm(lw, R("shi16", 0, 128), R("c16", j0, j0 + jn), True, True, jn)
+                else:
+                    for i in range(16):
+                        mm(lw, R("bigl", 15 - i, 143 - i), R1(sel, 1, v0 + i, v0 + n, 16), i == 0, i == 15, jn)
+                ts(lk, lw, float((U if last or ride else 0) + 1021 * (t + 1)), None, Alu.add, None, jn)
+
+                def part(r):
+                    return R(pn, r * V + v0, r * V + v0 + n)
+                tag[0] = "pg%d" % c
+                if CFG["ps"][c]:
+                    gather(CFG["pg"][c][0], part(rank), win, lk, n)
+                    arr = exchange(t + 1, c, part, 256 * n)[1]
+                else:
+                    arr = exchange(t + 1, c, lambda r: lists(t + 1, r, j0, j0 + jn), 16 * n)[1]
+                    for x, r in enumerate(ranks):
+                        gather(CFG["pg"][c][x], part(r), win, lists(t + 1, r, j0, j0 + jn), n, pad=0.0 if last or r == rank else CFG["pad"])
+                copies(t + 1, c, after=arr if c >= nc - 2 else [])
+            if not merge:
+                tag[0] = "ahl" if last else "ah%d" % c
+                bytes_of_winner()
+                to_lists(Q, 1 if last or ride else 2, 4)
+            for cs in CFG["reg"][t]:
+                if cs[-1] == c:
+                    banks = sorted(set(sum([qb[x] for x in cs if x < nc - 1], []))) + [Q] * last
+                    new_ends(cs, banks[:2] if len(banks) == 3 else banks[:4])
         if final:
-            mm(R("C0", 0, 64), M("I"), R1("pay", 0), True, False, 64)
-            mm(R("C0", 0, 64), M("I"), R1("pay", 1), False, True, 64)
-            act(R("ycf", 0, 64), R("C0", 0, 64), Act.Identity, 0.0, 1.0, 64)
-            act(R("yxf", 0, 64), R1("pay", 4), Act.Identity, 0.0, 1.0, 64)
+            tag[0] = "out"
+            ts(R("ycf", 0, 64), R("c16", 0, 64), 2048.0, None, Alu.add, None, 64)
             dma("S", "d_yc", ("yc", (full, full)), R("ycf", 0, 64)[:2], 32768, [R("ycf", 0, 64)], [])
             dma("S", "d_yx", ("yx", (full, full)), R("yxf", 0, 64)[:2], 32768, [R("yxf", 0, 64)], [])
     return ops
 
 
 def depend(ops):
-    hist, turns, deps = {}, {}, []
+    hist, turns, deps, group = {}, {}, [], {}
     for i, o in enumerate(ops):
         d = set()
         acc = [(r, False) for r in o["rd"]] + [(r, True) for r in o["wr"]]
@@ -327,13 +482,19 @@ def depend(ops):
             h = hist.setdefault(r[0], [])
             if wr and len(r[1]) == 2 and r[1][1].step is None:
                 h[:] = [e for e in h if not (r[2] <= e[1][2] and e[1][3] <= r[3])]
+            elif wr:
+                h[:] = [e for e in h if e[1][1] != r[1]]
             h.append((i, r, wr))
+        for k in list(d):
+            d.update(group.get(ops[k]["sem"], []))
+        if o["sem"] is not None:
+            group.setdefault(o["sem"], []).append(i)
         deps.append(sorted(d))
     return deps
 
 
 def times(o, P):
-    kind, n = o["cost"]
+    kind, n = o["cost"][:2]
     if kind == "v":
         c = max(64, n) * P["cyc"] + P["fix"]
     elif kind == "g":
@@ -345,7 +506,10 @@ def times(o, P):
     elif kind == "s":
         c = P["issue"] + (P["first"] if n else 0)
     elif kind == "x":
-        return 0.0, P["fly"]
+        return 0.0, P["fly"] + 3 * n / P["rbw"]
+    elif kind == "gd":
+        c = P["gissue"] * (2 if o["cost"][2] else 1)
+        return c, c + P["dlat"] + 2 * n / P["dbw"]
     else:
         return 60.0 + (n / P["dbw"] if o["eng"] == "Y" else 0.0), P["dlat"] + n / P["dbw"]
     return c, c
@@ -358,62 +522,64 @@ def gap(ops, k, i, P):
     return P["self"] if a == b and ops[k]["sem"] is None else P["lat"]
 
 
-def sweep(ops, tm, nxt, prio, back):
+def sweep(ops, tm, nxt, prio):
     n = len(ops)
-    left, ready, start = [0] * n, [0.0] * n, [0.0] * n
+    left, ready = [0] * n, [0.0] * n
     for i in range(n):
         for s, lag in nxt[i]:
             left[s] += 1
     cand = {e: [] for e in "VSPGYX"}
     free = {e: 0.0 for e in "VSPGYX"}
+    slack = [0.0 if o["tag"] in CFG["urgent"] else CFG["alpha"] for o in ops]
     for i in range(n):
         if not left[i]:
             cand[ops[i]["eng"]].append(i)
-    order = []
+    order, picks, stale = [], {}, set(cand)
     while len(order) < n:
-        best = None
-        for e in cand:
-            pick, limit = None, math.inf
-            for i in sorted(cand[e], key=lambda i: prio[i]):
-                st = max(ready[i] + (tm[i][1] - tm[i][0] if back else 0.0), free[e])
-                if pick is None or (st < pick[0] and st + tm[i][0] <= limit):
+        for e in stale:
+            pick, limit, f = (math.inf, -1), math.inf, free[e]
+            cand[e].sort(key=prio.get)
+            for i in cand[e]:
+                st = max(ready[i], f)
+                if st < pick[0] and st + tm[i][0] <= limit:
                     pick = (st, i)
-                limit = min(limit, st + 120.0)
-            if pick is not None and (best is None or pick < best):
-                best = pick
-        st, i = best
+                if st == f:
+                    break
+                limit = min(limit, st + 120.0 + slack[i] * (st - f))
+            picks[e] = pick
+        st, i = min(picks.values())
         e = ops[i]["eng"]
+        stale = {e}
         cand[e].remove(i)
         free[e] = st + tm[i][0]
-        start[i] = st
         order.append(i)
         for s, lag in nxt[i]:
-            ready[s] = max(ready[s], st + (tm[i][0] if back or lag is None else tm[i][1]) + (lag or 0.0))
+            ready[s] = max(ready[s], st + (tm[i][0] if lag is None else tm[i][1] + lag))
             left[s] -= 1
             if not left[s]:
                 cand[ops[s]["eng"]].append(s)
-    return order, start
+                stale.add(ops[s]["eng"])
+    return order
 
 
-def schedule(ops, deps, P, passes=3):
+def priority(ops, level, pri):
+    def place(o):
+        key = o["eng"] + o["tag"]
+        return pri.get(key + "F", pri.get(key, 90)) if o["round"] == RO - 1 else pri.get(key, 90)
+    return {i: (100 * o["round"] + place(o), i) if o["tag"] else (-1000 - level[i], i) for i, o in enumerate(ops)}
+
+
+def schedule(ops, deps, P):
     n = len(ops)
-    succ, pred = [[] for _ in range(n)], [[] for _ in range(n)]
+    succ = [[] for _ in range(n)]
     for i in range(n):
         for k, hard in [(k, True) for k in deps[i]] + [(k, ops[k]["eng"] != ops[i]["eng"]) for k in ops[i]["after"]]:
-            lag = gap(ops, k, i, P) + ops[i]["pad"] if hard else None
-            succ[k].append((i, lag))
-            pred[i].append((k, lag))
+            succ[k].append((i, gap(ops, k, i, P) + ops[i]["pad"] if hard else None))
     tm = [times(o, P) for o in ops]
     level = [0.0] * n
     for i in range(n - 1, -1, -1):
         level[i] = tm[i][1] + max([level[s] + (lag or 0.0) for s, lag in succ[i]] + [0.0])
-    order, start = sweep(ops, tm, succ, [-x for x in level], False)
-    best = (max(start[i] + tm[i][1] for i in range(n)), order)
-    for _ in range(passes):
-        back = sweep(ops, tm, pred, [-(start[i] + tm[i][1]) for i in range(n)], True)[1]
-        order, start = sweep(ops, tm, succ, [-(back[i] + tm[i][0]) for i in range(n)], False)
-        best = min(best, (max(start[i] + tm[i][1] for i in range(n)), order))
-    return best[1]
+    return sweep(ops, tm, succ, priority(ops, level, CFG["pri"]))
 
 
 def waits(ops, deps, order):
@@ -450,7 +616,7 @@ def rank_program(g, core, T, topo):
     rank = T.rank_of(core)
     if rank is None:
         return
-    ops = build(rank, CH, SHARE)
+    ops = build(rank)
     deps = depend(ops)
     order = schedule(ops, deps, NOMINAL)
     wl = waits(ops, deps, order)
@@ -476,6 +642,9 @@ def rank_program(g, core, T, topo):
     def ap(r):
         return T[r[0]][r[1]] if isinstance(r, tuple) else r
 
+    total = {}
+    for o in ops:
+        total[o["sem"]] = total.get(o["sem"], 0) + 16
     signal, cnt, sends = {}, {}, 0
     for i in order:
         o = ops[i]
@@ -496,9 +665,13 @@ def rank_program(g, core, T, topo):
                 g.sem_inc(T.sem["gi"], 1)
                 signal[i] = ("gi", cnt["gi"])
             continue
-        if kind == "dma":
-            q.dma_start(ap(c[1]), ap(c[2])).then_inc(T.sem[o["sem"]], 16)
-            signal[i] = (o["sem"], 16)
+        if kind in ("dma", "gd"):
+            if kind == "dma":
+                ins = q.dma_start(ap(c[1]), ap(c[2]))
+            else:
+                ins = q.dma_start(ap(c[1]), ap(c[2]), accum_op=Alu.add, max_dma_last_dim=4096)
+            ins.then_inc(T.sem[o["sem"]], 16)
+            signal[i] = (o["sem"], total[o["sem"]])
             continue
         if kind == "ts":
             if c[6] is None:
@@ -518,7 +691,7 @@ def rank_program(g, core, T, topo):
         elif kind == "gv":
             ins = q.tensor_copy(ap(c[1]), ap(c[2]).indirect(ap(c[3])))
         elif kind == "gs":
-            ins = q.activation(ap(c[1]), ap(c[2]).indirect(ap(c[3])), Act.Identity)
+            ins = q.activation(ap(c[1]), ap(c[2]).indirect(ap(c[3])), Act.Identity, scale=c[4])
         elif kind == "ge":
             ins = q.tensor_tensor(ap(c[1]), ap(c[2]).indirect(ap(c[3])), ap(c[4]), Alu.is_equal)
         elif c[4]:
@@ -530,6 +703,8 @@ def rank_program(g, core, T, topo):
             ins.then_inc(T.sem["s" + e], 1)
             signal[i] = ("s" + e, cnt[e])
     g.wait_ge(T.sem["sent"], sends * width[rank])
+    done = set(ops[i]["sem"] for i in waited)
     for i in order:
-        if ops[i]["sem"] is not None and i not in waited:
+        if ops[i]["sem"] is not None and ops[i]["sem"] not in done:
+            done.add(ops[i]["sem"])
             g.sync.wait_ge(T.sem[signal[i][0]], signal[i][1])

import math
from concourse.bass import DstId, RemoteDMATransfer
from concourse.mybir import AluOpType as Alu, ActivationFunctionType as Act

N, V, U, D, RO = 4, 1024, 4096, 16, 4
CFG = {
    "ch": [256, 128, 256, 256, 128],
    "nd": [[0, 0, 8, 7, 0]] * 4,
    "nq": [[0, 0, 0, 0, 0]] * 4,
    "rp": 2,
    "vm": [2, 2, 1, 1, 1],
    "ride": [[0, 0, 1, 1, 0]] * 4,
    "flv": 3, "qf": 1,
    "merge": [[1, 1, 1, 0, 1]] * 4,
    "ps": [0, 0, 0, 0, 0],
    "pg": ["SSSS", "SSSS", "SSSS", "SVSS", "VSVV"],
    "reg": [[[0, 1], [2, 3], [4]]] * 4,
    "ob": [3, 0, 0, 1, 0], "lastb": [0, 1], "nef": 0,
    "pad": 0.0, "dpad": 0.0, "alpha": 1.0, "urgent": ["sel4", "cnt4", "pg4"],
    "pri": {'Ggs2': 6, 'Ggs3': 7, 'Gpg0': 15, 'Gpg1': 37, 'Gpg2': 6, 'Gpg3': 5, 'Gpg4': 16, 'Pah0': 30, 'Pah1': 88, 'Pah4': 31, 'Pcnt0': 22,
            'Pcnt1': 15, 'Pcnt2': 14, 'Pcnt3': 18, 'Pcnt4': 29, 'Pne0': 34, 'Pne2': 67, 'Pne4': 14, 'Psel0': 9, 'Psel1': 13, 'Psel2': 17,
            'Psel3': 2, 'Psel4': 52, 'Sgs2': 4, 'Sgs3': 17, 'Sne0': 17, 'Sne2': 2, 'Sne4': 23, 'Spg0': 19, 'Spg1': 16, 'Spg2': 95, 'Spg3': 18,
            'Spg4': 5, 'Ssel0': 48, 'Ssel1': 23, 'Ssel2': -21, 'Ssel3': 7, 'Ssel4': 54, 'Vcmp2': 2, 'Vcmp3': -51, 'Vge0': 10, 'Vge1': 11,
            'Vge3': 12, 'Vge4': 13, 'Vhalf': 69, 'Vne0': 55, 'Vne2': -51, 'Vne4': 49, 'Vpg3': 9, 'Vpg4': -52, 'Vsel0': 23, 'Vsel1': 1,
            'Vsel2': -27, 'Vsel3': -30, 'Vsel4': 10},
}
CFG["pri"] = {'Ggs2':20,'Ggs3':17,'Gpg0':-16,'Gpg1':18,'Gpg2':3,'Gpg3':-25,'Gpg4':22,'Pah0':49,'Pah1':95,'Pah4':21,'Pcnt0':76,'Pcnt1':95,'Pcnt2':96,'Pcnt3':28,'Pcnt4':39,'Pne0':40,'Pne2':85,'Pne4':111,'Psel0':23,'Psel1':3,'Psel2':33,'Psel3':-15,'Psel4':45,'Sgs2':21,'Sgs3':28,'Sne0':19,'Sne2':26,'Sne4':21,'Spg0':89,'Spg1':25,'Spg2':60,'Spg3':23,'Spg4':24,'Ssel0':59,'Ssel1':1,'Ssel2':33,'Ssel3':13,'Ssel4':80,'Vcmp2':0,'Vcmp3':12,'Vge0':-19,'Vge1':11,'Vge3':11,'Vge4':18,'Vhalf':22,'Vne0':23,'Vne2':24,'Vne4':23,'Vpg3':-11,'Vpg4':10,'Vsel0':28,'Vsel1':2,'Vsel2':17,'Vsel3':-5,'Vsel4':0,'Pahl':54,'Pout':54,'Sahl':0,'Sout':21,'Vahl':22,'Yne4':-27,'Ypg0':12,'Ypg1':17,'Ypg2':-26,'Ypg3':12,'Ypg4':13,'Vhalf0':61,'Pah0F':107,'Pah1F':52,'Pah4F':83,'Pcnt0F':110,'Pcnt1F':109,'Pcnt2F':101,'Pcnt3F':92,'Pcnt4F':92,'Pne0F':131,'Pne2F':60,'Pne4F':98,'PoutF':116,'Psel0F':74,'Psel1F':105,'Psel2F':96,'Psel3F':66,'Psel4F':59,'Sgs2F':-1,'Sgs3F':97,'Sne0F':-55,'Sne2F':-43,'Sne4F':5,'SoutF':-52,'Ssel0F':68,'Ssel1F':96,'Ssel2F':98,'Ssel3F':10,'Ssel4F':69,'Vcmp2F':-62,'Vcmp3F':6,'Vge0F':-67,'Vge1F':-68,'Vge3F':-7,'Vge4F':-34,'VhalfF':-13,'Vne0F':-53,'Vne2F':-67,'Vne4F':-41,'Vsel2F':7,'Vsel3F':-93,'Vsel4F':36}
CFG.update(reg=[[[0,1,2],[3,4]]]*4,pg=["SSSS","SSSS","SSSS","SSSS","VSVV"], pri={'Ggs2':-55,'Ggs3':-89,'Gpg0':-90,'Gpg1':-91,'Gpg2':-47,'Gpg3':-99,'Gpg4':-32,'Pah0':81,'Pah1':78,'Pah4':80,'Pcnt0':126,'Pcnt1':13,'Pcnt2':32,'Pcnt3':60,'Pcnt4':73,'Pne0':108,'Psel0':12,'Psel1':48,'Psel2':59,'Psel3':39,'Psel4':55,'Sgs2':12,'Sgs3':13,'Sne0':-6,'Spg0':65,'Spg1':64,'Spg2':13,'Spg3':82,'Spg4':83,'Ssel0':64,'Ssel1':64,'Ssel2':22,'Ssel3':-10,'Ssel4':-36,'Vcmp2':20,'Vcmp3':5,'Vge0':-6,'Vge1':-16,'Vge3':13,'Vge4':49,'Vhalf':78,'Vne0':37,'Vpg4':48,'Vsel0':-7,'Vsel1':30,'Vsel2':13,'Vsel3':10,'Vsel4':-11,'Pahl':79,'Sahl':16,'Sout':7,'Vahl':79,'Ypg0':-53,'Ypg1':-55,'Ypg2':-28,'Ypg3':-55,'Ypg4':-27,'Vhalf0':79,'Pah3':56,'Vah3':93,'Sah3':8,'Pne3':111,'Sne3':-7,'Vne3':49,'Vout':50,'Yne3':-16})
CFG.update(sgs=[0] * 5, ch=[384,256,256,128],nd=[[0,8,7,0]]*4,nq=[[0]*4]*4,vm=[1,1,1,1],ride=[[0,1,1,0]]*4,merge=[[1,1,0,0]]*4,ps=[0]*4,pg=["SSSS","SSSS","SSSS","VSVV"],reg=[[[0,1],[2,3]]]*4,lastb=[3,0],urgent=["sel3","cnt3","pg3"])
CFG["pri"] = {'Ggs1':-137,'Ggs2':-132,'Gpg0':-137,'Gpg1':-128,'Gpg2':-136,'Gpg3':-135,'Pah0':90,'Pah3':76,'Pcnt0':89,'Pcnt1':45,'Pcnt2':53,'Pcnt3':69,'Pne0':69,'Psel0':17,'Psel1':45,'Psel2':-2,'Psel3':67,'Sgs1':135,'Sgs2':151,'Sne0':129,'Spg0':231,'Spg1':139,'Spg2':141,'Spg3':153,'Ssel0':128,'Ssel1':147,'Ssel2':119,'Ssel3':146,'Vcmp1':44,'Vcmp2':-66,'Vge0':9,'Vge2':19,'Vge3':83,'Vhalf':-44,'Vne0':18,'Vpg3':-69,'Vsel0':-70,'Vsel1':-53,'Vsel2':-43,'Vsel3':15,'Pahl':39,'Sahl':150,'Sout':130,'Vahl':15,'Ypg0':21,'Ypg1':18,'Ypg2':-5,'Ypg3':2,'Vhalf0':-80,'Pah2':68,'Vah2':37,'Sah2':140,'Pne2':91,'Sne2':149,'Vne2':19,'Vout':-46,'Yne2':25,'Pah0F':31,'Pah3F':121,'Pcnt0F':130,'Pcnt1F':142,'Pcnt2F':120,'Pcnt3F':105,'Pne0F':129,'Pne2F':123,'Psel0F':129,'Psel1F':9,'Psel2F':49,'Psel3F':53,'Sgs1F':81,'Sgs2F':123,'Sne0F':122,'Sne2F':173,'SoutF':82,'Ssel0F':67,'Ssel1F':123,'Ssel2F':52,'Ssel3F':113,'Vcmp1F':33,'Vcmp2F':120,'Vge0F':15,'Vge2F':56,'Vge3F':147,'VhalfF':21,'Vne0F':44,'Vne2F':46,'VoutF':70,'Vsel1F':75,'Vsel2F':22,'Vsel3F':32}
BETA = 0.598
BIG = 1048576.0
FW = 11264
MATS = ["I", "I128", "nI", "nM", "M2", "Kp", "DM", "ShI"] + ["%s%d" % (a, j) for a in ("Wd", "Wr") for j in range(8)]
MATS += ["K%d" % t for t in range(RO)]
SCALED = {"I128": 128.0, "nI": -1.0, "nM": -BIG, "M2": 2 * BIG}
for _j in range(8):
    SCALED["Wr%d" % _j] = 1.0 - 2.0 ** (-1 - _j)
    SCALED["Wd%d" % _j] = 2.0 ** (7 - _j)

SCRATCH = {
    "fam3": ("sbuf", [128, FW], "bfloat16"),
    "ow0": ("sbuf", [128, 8 * V], "bfloat16"), "ow1": ("sbuf", [128, 8 * V], "bfloat16"),
    "eq": ("sbuf", [128, D * V], "bfloat16"),
    "offs": ("sbuf", [128, 1024], "uint16"), "look": ("sbuf", [128, RO * N * 64], "uint16"),
    "bi": ("sbuf", [128, D, 64], "int32"), "w": ("sbuf", [128, D, 64], "int32"), "b16": ("sbuf", [128, D, 64], "float16"),
    "b": ("sbuf", [128, D, 64], "float32"),
    "ca": ("sbuf", [128, 64], "int32"), "cb": ("sbuf", [128, 64], "int32"),
    "cs": ("sbuf", [128, 64], "int32"), "ct": ("sbuf", [128, 64], "int32"),
    "ci": ("sbuf", [128, 8], "int32"), "cf": ("sbuf", [128, 32], "float32"),
    "colf": ("sbuf", [128, 144], "float32"), "colg": ("sbuf", [128, 128], "float32"),
    "cm": ("sbuf", [128, 128 * len(MATS)], "bfloat16"), "tmpm": ("sbuf", [128, 144], "bfloat16"),
    "tmpn": ("sbuf", [128, 128], "bfloat16"), "tmpo": ("sbuf", [128, 128], "bfloat16"),
    "big": ("sbuf", [128, 144], "bfloat16"), "bigl": ("sbuf", [128, 144], "float16"),
    "big16": ("sbuf", [128, 144], "float16"), "h37": ("sbuf", [128, 128], "float16"), "h101": ("sbuf", [128, 128], "float16"),
    "shi16": ("sbuf", [128, 128], "float16"), "c16": ("sbuf", [128, 64], "float16"), "tmpf": ("sbuf", [128, 128], "float32"),
    "kt": ("sbuf", [128, D, 64], "bfloat16"), "kc": ("sbuf", [128, D, 64], "bfloat16"), "fl": ("sbuf", [128, 14, 64], "bfloat16"),
    "pay": ("sbuf", [128, 4, 64], "bfloat16"), "sel": ("sbuf", [128, 4, V], "bfloat16"), "sel16": ("sbuf", [128, 4, V], "float16"),
    "cl": ("sbuf", [128, 2, 64], "bfloat16"), "fr": ("sbuf", [128, 2, 64], "float32"),
    "cq": ("sbuf", [128, 2 * V], "bfloat16"), "sg": ("sbuf", [128, V], "bfloat16"), "ww": ("sbuf", [128, V], "bfloat16"),
    "ycf": ("sbuf", [128, 64], "float32"), "yxf": ("sbuf", [128, 64], "float32"),
}
for _t in range(RO):
    SCRATCH["pa%d" % _t] = ("sbuf", [128, U], "bfloat16")
    SCRATCH["Q%d" % _t] = ("psum", [128, 512], "float32")
    SCRATCH["X%d" % _t] = ("psum", [128, 512], "float32")

SEMAPHORES = ["sV", "sS", "sP", "sG", "gi", "sent",
              "d_ca", "d_cb", "d_cc", "d_fam", "d_nb", "d_f2", "d_f3", "d_yc", "d_yx", "d_y0", "d_y1", "d_y2", "d_y3"]
SEMAPHORES += ["a0_0_%d" % r for r in range(N)]
SEMAPHORES += ["a%d_%d_%d" % (t, c, r) for t in range(1, RO) for c in range(5) for r in range(N)]
SEMAPHORES += ["o%d_%d" % (t, c) for t in range(RO) for c in range(5)]
SEMAPHORES += ["g%d" % i for i in range(44)]

NOMINAL = {"cyc": 1.0, "pe": 0.5, "gam": 1.56, "lat": 110.0, "self": 60.0, "fix": 30.0, "issue": 900.0, "fly": 3000.0, "first": 2500.0,
           "dlat": 2000.0, "dbw": 260.0, "gissue": 1000.0, "rbw": 60.0}


def R(name, a, b, step=1):
    return (name, (slice(None), slice(a, b, step) if step != 1 else slice(a, b)), a, b)


def R3(name, k0, k1, j0=0, j1=None, step=1):
    w = SCRATCH[name][1][2]
    j1 = w if j1 is None else j1
    return (name, (slice(None), slice(k0, k1), slice(j0, j1, step) if step != 1 else slice(j0, j1)), k0 * w + j0, (k1 - 1) * w + j1, j0, j1)


def R1(name, k, j0=0, j1=None, step=1):
    w = SCRATCH[name][1][2]
    j1 = w if j1 is None else j1
    return (name, (slice(None), k, slice(j0, j1, step) if step != 1 else slice(j0, j1)), k * w + j0, k * w + j1, j0, j1)


def meet(r, s):
    return r[2] < s[3] and s[2] < r[3] and (len(r) < 6 or len(s) < 6 or (r[4] < s[5] and s[4] < r[5]))


def M(name):
    i = MATS.index(name)
    return R("cm", 128 * i, 128 * i + 128)


def wide(r):
    return SCRATCH[r[0]][2] in ("float32", "int32")


def in_psum(r):
    return SCRATCH[r[0]][0] == "psum"


def build(rank):
    ops = []
    ch, rp = CFG["ch"], CFG["rp"]
    nc = len(ch)
    at = [sum(ch[:c]) for c in range(nc + 1)]
    full = slice(None)
    qb, nb = [], 0
    for n in ch[:-1]:
        qb.append(["Q%d" % nb, "Q%d" % (nb + (n > 256))])
        nb += 1 + (n > 256)
    ngd, tag = [0], ["", -1]

    def add(eng, call, cost, rd, wr, after=(), pad=0.0, sem=None):
        ops.append({"eng": eng, "call": call, "cost": cost, "rd": list(rd), "wr": list(wr), "after": list(after), "pad": pad, "sem": sem,
                    "tag": tag[0], "round": tag[1]})
        return len(ops) - 1

    def aps(*xs):
        return [x for x in xs if isinstance(x, tuple)]

    def ts(out, a, s1, s2, o0, o1, n, **k):
        return add("V", ("ts", out, a, s1, s2, o0, o1), ("v", n * (1.0 if wide(out) or wide(a) else 0.5)), aps(a, s1, s2), [out], **k)

    def tt(out, a, b, op, n, **k):
        return add("V", ("tt", out, a, b, op), ("v", n * (1.0 if in_psum(a) or in_psum(b) else 2.0)), [a, b], [out], **k)

    def cp(out, a, n, **k):
        return add("V", ("cp", out, a), ("v", n * (1.0 if wide(out) or wide(a) else 0.5)), [a], [out], **k)

    def act(out, a, f, bias, scale, n, **k):
        return add("S", ("act", out, a, f, bias, scale), ("v", n), aps(a, bias, scale), [out], **k)

    def mm(out, lhs, rhs, start, stop, n, **k):
        return add("P", ("mm", out, lhs, rhs, start, stop), ("p", max(64, n)), [lhs, rhs], [out], **k)

    def gather(eng, out, win, off, n, scale=1.0, **k):
        return add(eng, ("gv" if eng == "V" else "gs", out, win, off, scale), ("g", n), [win, off], [out], **k)

    def dma(q, sem, out, a, nbytes, rd, wr, **k):
        return add(q, ("dma", out, a), ("d", nbytes), rd, wr, sem=sem, **k)

    def lists(t, r, j0, j1):
        return R("look", (t * N + r) * 64 + j0, (t * N + r) * 64 + j1)

    def exchange(t, c, what, nbytes):
        s = add("G", ("send", what(rank), "a%d_%d_%d" % (t, c, rank)), ("s", t == 0), [what(rank)], [])
        return s, [add("X", ("arr",), ("x", nbytes), [], [what(r)], after=[s], sem="a%d_%d_%d" % (t, c, r)) for r in range(N) if r != rank]

    def to_offsets(k0, k1, c):
        v0, jn = at[c], ch[c] // 16
        off = R("offs", v0 + k0 * jn, v0 + k1 * jn)
        cp(off, R3("bi", k0, k1, v0 // 16, v0 // 16 + jn), (k1 - k0) * jn)
        was = list(tag)
        tag[:] = ["half" if was[0] else "half0", tag[1] + 1]
        ts(R3("b16", k0, k1, v0 // 16, v0 // 16 + jn), off, -2048.0, None, Alu.add, None, (k1 - k0) * jn)
        tag[:] = was

    def copies(t, c, **k):
        n, v0 = ch[c], at[c]
        src = R("pa%d" % t, rank * V + v0, rank * V + v0 + n)
        for h in range(2 * max(min(rp, CFG["nd"][t][c]), CFG["vm"][c])):
            o2 = R("ow%d" % (t % 2), 8 * v0 + h * n, 8 * v0 + h * n + n)
            dma("Y", "o%d_%d" % (t, c), o2[:2], src[:2], 256 * n, [src], [o2], **k)

    def cf(i):
        return R("cf", i, i + 1)

    ranks = [rank] + [q for q in range(N) if q != rank]
    dma("Y", "d_ca", ("ca", (full, full)), ("c0", (full, full)), 32768, [], [R("ca", 0, 64)])
    dma("S", "d_cb", ("cb", (slice(0, 112), full)), ("c0", (slice(16, 128), full)), 28672, [], [R("cb", 0, 32)])
    dma("S", "d_cc", ("cb", (slice(112, 128), full)), ("c0", (slice(0, 16), full)), 4096, [], [R("cb", 32, 64)])
    dma("Y", "d_fam", ("fam3", (full, slice(0, U))), ("fam", (full, full)), 1 << 20, [], [R("fam3", 0, U)])
    add("G", ("iota", R("ci", 0, 2), [[112, 2]], 1, False), ("i", 2), [], [R("ci", 0, 2)])
    add("G", ("iota", R("colf", 0, 144), [[1, 144]], 0, True), ("i", 144), [], [R("colf", 0, 144)])
    add("G", ("iota", R("colg", 0, 128), [[16, 8], [0, 16]], 0, True), ("i", 128), [], [R("colg", 0, 128)])
    tt(R("cs", 0, 64), R("ca", 0, 64), R("cb", 0, 64), Alu.add, 64)
    ts(R("ct", 0, 64), R("cs", 0, 64), U - 1, None, Alu.bitwise_and, None, 64)
    cp(lists(0, rank, 0, 64), R("ct", 0, 64), 64)
    s0, arr0 = exchange(0, 0, lambda r: lists(0, r, 0, 64), 16384)
    add("G", ("iota", R3("kc", 0, D), [[1, D], [0, 64]], 1, True), ("i", 1024), [], [R3("kc", 0, D)], after=[s0])
    dma("S", "d_nb", ("bi", (full, full, full)), ("nb", (full, full)), 1 << 19, [], [R("bi", 0, 1024)])
    ts(R("ci", 2, 4), R("ci", 0, 2), 112, None, Alu.bitwise_and, None, 2)
    ts(R("ci", 4, 5), R("ci", 1, 2), 127, None, Alu.bitwise_and, None, 1)
    ts(R("ci", 5, 6), R("ci", 0, 1), 15, None, Alu.bitwise_and, None, 1)
    cp(R("cf", 0, 6), R("ci", 0, 6), 6)
    ts(R("cf", 6, 8), R("cf", 2, 4), 15.0, None, Alu.add, None, 2)
    ts(cf(8), cf(5), -BETA, 81.0, Alu.mult, Alu.add, 1)
    ts(cf(9), cf(5), -BETA, 81.0 + 16 * BETA * 256, Alu.mult, Alu.add, 1)
    ts(cf(10), cf(5), 128.0, None, Alu.mult, None, 1)
    ts(cf(11), cf(5), 256.0, None, Alu.mult, None, 1)
    ts(M("I"), R("colf", 0, 128), cf(0), None, Alu.is_equal, None, 128)
    for name in SCALED:
        act(M(name), M("I"), Act.Identity, 0.0, SCALED[name], 128)
    ts(R("h37", 0, 128), M("I"), 37.0, None, Alu.mult, None, 128)
    ts(R("h101", 0, 128), M("I"), 101.0, None, Alu.mult, None, 128)
    ts(R("tmpn", 0, 128), R("colg", 0, 128), cf(2), -0.4, Alu.is_equal, Alu.mult, 128)
    tt(M("DM"), R("tmpn", 0, 128), M("I"), Alu.add, 128)
    ts(R("tmpo", 0, 128), R("colf", 0, 128), cf(4), None, Alu.is_equal, None, 128)
    tt(M("ShI"), R("tmpo", 0, 128), M("I"), Alu.add, 128)
    cp(R("shi16", 0, 128), M("ShI"), 128)
    ts(R("big", 0, 144), R("colf", 0, 144), cf(6), None, Alu.is_equal, None, 144)
    ts(R("tmpm", 0, 144), R("colf", 0, 144), cf(7), None, Alu.is_equal, None, 144)
    cp(R("big16", 0, 144), R("big", 0, 144), 144)
    tt(R("bigl", 0, 144), R("tmpm", 0, 144), R("big", 0, 144), Alu.add, 144)
    for k0, k1, val in ((0, 2, -129.0), (2, 14, 129.0), (14, 16, 258.0)):
        add("V", ("ms", R3("kt", k0, k1), val), ("v", (k1 - k0) * 32), [], [R3("kt", k0, k1)])
    ts(cf(12), cf(0), 0.0, 768.0, Alu.is_equal, Alu.mult, 1)
    ts(cf(13), cf(0), 1.0, None, Alu.is_equal, None, 1)
    ts(cf(14), cf(0), 2.0, None, Alu.is_equal, None, 1)
    ts(cf(15), cf(13), 86.0, cf(12), Alu.mult, Alu.add, 1)
    ts(cf(16), cf(14), -43.0, cf(15), Alu.mult, Alu.add, 1)
    ts(cf(24), cf(0), 3.0, -70.0 * U, Alu.is_equal, Alu.mult, 1)
    ts(cf(25), cf(0), 4.0, 70.0 * U, Alu.is_equal, Alu.mult, 1)
    ts(cf(26), cf(16), cf(24), cf(25), Alu.add, Alu.add, 1)
    ts(cf(17), cf(14), cf(13), None, Alu.subtract, None, 1)
    for t in range(RO):
        ts(cf(18 + t), cf(17), float(t), cf(26), Alu.mult, Alu.add, 1)
        act(M("K%d" % t), M("I"), Act.Identity, cf(18 + t), 0.0, 128)
    ts(cf(22), cf(0), 0.0, cf(13), Alu.is_equal, Alu.subtract, 1)
    tt(R("tmpf", 0, 128), R("colg", 0, 128), R("colf", 0, 128), Alu.subtract, 128)
    ts(R("tmpf", 0, 128), R("tmpf", 0, 128), 256.0, 2048.0, Alu.mult, Alu.add, 128)
    ts(M("Kp"), R("tmpf", 0, 128), cf(22), None, Alu.mult, None, 128)
    for r in ranks:
        for h, eng in enumerate("VS"):
            gather(eng, R("pa0", r * V + 512 * h, r * V + 512 * h + 512), R("fam3", 0, U), lists(0, r, 32 * h, 32 * h + 32), 512)
    for c in range(nc):
        copies(0, c)
    for c in range(nc):
        to_offsets(0, D, c)
    dma("Y", "d_f2", ("fam3", (full, slice(U, 2 * U))), ("fam", (full, full)), 1 << 20, [], [R("fam3", U, 2 * U)], after=arr0)
    dma("Y", "d_f3", ("fam3", (full, slice(2 * U, FW))), ("fam", (full, slice(0, FW - 2 * U))), 256 * (FW - 2 * U), [], [R("fam3", 2 * U, FW)], after=arr0)
    win = R("fam3", 0, FW)

    for t in range(RO):
        final = t == RO - 1
        tag[1] = t
        ow, pn = "ow%d" % (t % 2), "pa%d" % (t + 1)
        pall = R("pa%d" % t, 0, U)

        def new_ends(cs, banks):
            ja, jb = at[cs[0]] // 16, at[cs[-1] + 1] // 16
            jw = jb - ja
            tag[0] = "ne%d" % cs[0]
            for j in range(7):
                if final and jb == 64 and j < CFG["flv"]:
                    ts(R3("fl", 2 * j, 2 * j + 2, ja, jb), R3("pay", 2, 4, ja, jb), 2.0 ** (j - 7), 128.502, Alu.mult, Alu.add, 2 * jw)
                else:
                    act(R3("fl", 2 * j, 2 * j + 2, ja, jb), R3("pay", 2, 4, ja, jb), Act.Identity, 128.502, 2.0 ** (j - 7), 2 * jw)
            je = at[max([c + 1 for c in cs if c < nc - 1 and not CFG["ride"][t][c]] + [cs[0]])] // 16
            if ja < je:
                cw = R(banks[0], 448, 448 + je - ja)
                for h in range(2):
                    mm(cw, M("I"), R1("pay", h, ja, je), h == 0, h == 1, je - ja)
                ts(R("c16", ja, je), cw, -2048.0, None, Alu.add, None, je - ja)
            kq = D // len(banks)
            for q, Z in enumerate(banks):
                k0, k1, wd = kq * q, kq * q + kq, kq * jw

                def zs(a, b):
                    return R(Z, jw * (a - k0), jw * (b - k0))
                zq = zs(k0, k1)
                bq, wq, iq = [R3(x, k0, k1, ja, jb) for x in ("b", "w", "bi")]
                ka, kb = max(k0, 2), min(k1, 14)
                mm(zq, M("nM"), R3("kt", k0, k1, ja, jb), True, False, wd)
                mm(zs(k0, kb), M("nM"), R3("fl", k0, kb, ja, jb), False, False, jw * (kb - k0))
                mm(zs(ka, k1), M("M2"), R3("fl", ka - 2, k1 - 2, ja, jb), False, False, jw * (k1 - ka))
                for k in range(max(k0, 14), k1):
                    mm(zs(k, k + 1), M("nM"), R1("pay", k - 12, ja, jb), False, False, jw)
                mm(zq, M("K%d" % t), R3("kc", k0, k1, ja, jb), False, False, wd)
                for k in range(k0, k1):
                    mm(zs(k, k + 1), R("h101", 0, 128), R("c16", ja, jb), False, False, jw)
                mm(zq, R("h37", 0, 128), R3("b16", k0, k1, ja, jb), False, True, wd)
                tt(wq, zq, iq, Alu.max, wd)
                ts(iq, wq, U - 1, None, Alu.bitwise_and, None, wd)
                if final:
                    cp(bq, iq, wd)
                    if jb == 64:
                        for x in range(k0 // 4, k1 // 4):
                            dma("YS"[x % 2], "d_y%d" % x, ("yn", (full, slice(256 * x, 256 * x + 256))), R3("b", 4 * x, 4 * x + 4)[:2], 1 << 17,
                                [R3("b", 4 * x, 4 * x + 4)], [])
                elif k1 % 8 == 0 and cs[0] == 0:
                    to_offsets(k1 - max(8, kq), k1, 0)
            if final:
                Z = banks[0]
                for k in range(16):
                    mm(R(Z, 448, 448 + jw), M("I" if k < 2 else "nI"), R1("pay", 2 + k, ja, jb) if k < 2 else R1("fl", k - 2, ja, jb), k == 0, k == 15, jw)
                act(R("yxf", ja, jb), R(Z, 448, 448 + jw), Act.Identity, 14 * 129.0, 1.0, jw)
            else:
                for c in cs:
                    if c:
                        to_offsets(0, D, c)

        for c, n in enumerate(ch):
            v0 = at[c]
            jn, j0, last, nd, nq, vm = n // 16, v0 // 16, c == nc - 1, CFG["nd"][t][c], CFG["nq"][t][c], CFG["vm"][c]
            C, Q = ("X%d" % CFG["lastb"][0], "X%d" % CFG["lastb"][1]) if last else ("X%d" % c, qb[c][0])
            ride, merge = CFG["ride"][t][c], final or (CFG["merge"][t][c] and not last)
            O = Q if last else C
            O2 = C if ride else "X%d" % CFG["ob"][c]
            sel, big = ("sel16", "big16") if ride or last else ("sel", "big")
            ww, sg = R("ww", v0, v0 + n), R("sg", v0, v0 + n)

            def own(m):
                return R(ow, 8 * v0, 8 * v0 + m * n)

            def pair(j, m=1):
                return R("eq", D * v0 + 2 * n * j, D * v0 + 2 * n * (j + m))

            def poff(j, m=1):
                return R("offs", v0 + 2 * jn * j, v0 + 2 * jn * (j + m))

            def colours():
                mm(R(O, 0, n), M("I"), own(1), True, False, n)
                for a in range(0, n, 128):
                    b = min(n, a + 128)
                    mm(R(O, a, b), M("Kp"), R3("kc", 0, 2, 0, (b - a) // 2), False, b == n, b - a)

            def ah(h):
                return R(O, n + h * n, 2 * n + h * n) if last else R(qb[c][h], 0, n) if n > 256 else R(Q, h * n, h * n + n)
            tag[0] = "cnt%d" % c
            if last:
                colours()
            if nq:
                mm(R(O2, 0, 2 * n), M("I"), own(2), True, True, 2 * n)
            tag[0] = "gs%d" % c
            for j in range(0, nd, rp):
                m = min(rp, nd - j)
                gather("S", pair(j, m), pall, poff(j, m), 2 * n * m, -1.0)
                add("G", ("gd", pair(j, m), own(2 * m)), ("gd", 512 * n * m, ngd[0] == 0), [own(2 * m), pair(j, m)], [pair(j, m)], sem="g%d" % ngd[0])
                ngd[0] += 1
            for j in range(nd, nd + nq):
                gather("S", pair(j), pall, poff(j), 2 * n)
            late = max(0, nd - CFG["qf"] * rp) // rp * rp
            for i, j in enumerate(list(range(nd + nq, 8)) + list(range(late)) + list(range(nd, nd + nq)) + list(range(late, nd))):
                tag[0] = ("ge%d" if j >= nd + nq else "cmp%d") % c
                if j >= nd + nq:
                    if (7 - j) % vm == vm - 1 or j == nd + nq:
                        m = (7 - j) % vm + 1
                        add("V", ("ge", pair(j, m), pall, poff(j, m), own(2 * m)), ("g", 2 * n * m), [pall, poff(j, m), own(2 * m)], [pair(j, m)])
                elif j >= nd:
                    tt(pair(j), pair(j), R(O2, 0, 2 * n), Alu.is_equal, 2 * n, pad=150.0)
                elif j % rp == 0:
                    m = min(rp, nd - j)
                    ts(pair(j, m), pair(j, m), 0.0, None, Alu.is_equal, None, 2 * n * m, pad=CFG["dpad"])
                e0 = D * v0 + 2 * n * j
                tag[0] = "cnt%d" % c
                if ride:
                    mm(R(Q, 0, 2 * n), M("Wr%d" % j), pair(j), i == 0, i == 7, 2 * n)
                else:
                    mm(R(C, 0, n), M("I"), R("eq", e0, e0 + n), i == 0, False, n)
                    mm(R(C, 0, n), M("I"), R("eq", e0 + n, e0 + 2 * n), False, i == 7, n)
                    tag[0] = "ah%d" % c
                    if n > 256:
                        for h in range(2):
                            mm(ah(h), M("Wd%d" % j), R("eq", e0 + h * n, e0 + h * n + n), i == 0, False, n)
                    else:
                        mm(R(O, n, 3 * n) if last else R(Q, 0, 2 * n), M("Wd%d" % j), pair(j), i == 0, last and i == 7, 2 * n)
            tag[0] = "sel%d" % c
            lk = None if final else lists(t + 1, rank, j0, j0 + jn)
            cw = R(C, 256, 256 + n) if ride else R(C, 0, n)
            if ride:
                cq = R("cq", 2 * v0, 2 * v0 + 2 * n)
                colours()
                act(cq, R(Q, 0, 2 * n), Act.Identity, 128.498, 1.0, 2 * n)
                for h in range(2):
                    mm(cw, M("I"), R("cq", 2 * v0 + h * n, 2 * v0 + h * n + n), h == 0, h == 1, n)
            if last or ride:
                act(ww, cw, Act.Exp, cf(9 if ride else 8), -16 * BETA, n)
                mm(cw, M("DM"), ww, True, True, n)
                if CFG["sgs"][c]:
                    act(ww, cw, Act.Sign, 0.0, 1.0, n)
                    act(sg, ww, Act.Identity, 0.5, 0.5, n)
                else:
                    ts(sg, cw, 0.0, None, Alu.is_gt, None, n)
                tt(R1(sel, 1, v0, v0 + n), R(O, 0, n), sg, Alu.mult, n)
            else:
                act(ww, R(C, 0, n), Act.Exp, cf(8), -16 * BETA, n)
                mm(R(C, 0, n), M("DM"), ww, True, True, n)
                act(sg, R(C, 0, n), Act.Sign, 0.0, 1.0, n)
                mm(R(O, 0, n), M("I"), own(1), True, False, n)
                mm(R(O, 0, n), M("I128"), sg, False, True, n)
                act(R1("sel", 1, v0, v0 + n), sg, Act.Identity, cf(10), cf(10), n)
                act(R1("sel", 0, v0, v0 + n), R(O, 0, n), Act.Relu, -128.0, 1.0, n)

            def bytes_of_winner():
                for h in range(2):
                    if ride or last:
                        tt(R1(sel, 2 + h, v0, v0 + n), ah(h), sg, Alu.mult, n)
                    else:
                        mm(ah(h), M("I128"), sg, False, h == 1 or n > 256, n)
                        if n > 256:
                            act(R1(sel, 2 + h, v0, v0 + n), ah(h), Act.Relu, -128.0, 1.0, n)
                if not (ride or last or n > 256):
                    act(R3(sel, 2, 4, v0, v0 + n), R(Q, 0, 2 * n), Act.Relu, -128.0, 1.0, 2 * n)

            def to_lists(bank, a, b):
                for i in range(16):
                    mm(R(bank, 0, (b - a) * jn), R(big, 15 - i, 143 - i), R3(sel, a, b, v0 + i, v0 + n, 16), i == 0, i == 15, (b - a) * jn)
                if not (last or ride):
                    act(R3("pay", a, b, j0, j0 + jn), R(bank, 0, (b - a) * jn), Act.Identity, 0.0, 1.0, (b - a) * jn)
                    return
                cp(R("c16", j0, j0 + jn), R(bank, 0, jn), jn)
                qs, cl, fr = R(bank, jn, 3 * jn), R3("cl", 0, 2, j0, j0 + jn), R3("fr", 0, 2, j0, j0 + jn)
                if last:
                    act(R3("pay", 2, 4, j0, j0 + jn), qs, Act.Identity, 0.0, 1.0, 2 * jn)
                else:
                    act(cl, qs, Act.Identity, 128.498, 1.0, 2 * jn)
                    tt(fr, qs, cl, Alu.subtract, 2 * jn)
                    act(R3("pay", 2, 4, j0, j0 + jn), fr, Act.Identity, -32768.0, -256.0, 2 * jn)
            if merge:
                bytes_of_winner()
            if merge or not (last or ride):
                to_lists(O, 1 if last or ride else 0, 4 if merge else 2)
            if not final:
                lw = R(C, 448, 448 + jn)
                if not (last or ride):
                    for h in range(2):
                        mm(lw, M("ShI"), R1("pay", h, j0, j0 + jn), h == 0, h == 1, jn)
                elif merge:
                    mm(lw, R("shi16", 0, 128), R("c16", j0, j0 + jn), True, True, jn)
                else:
                    for i in range(16):
                        mm(lw, R("bigl", 15 - i, 143 - i), R1(sel, 1, v0 + i, v0 + n, 16), i == 0, i == 15, jn)
                ts(lk, lw, float((U if last or ride else 0) + 1021 * (t + 1)), None, Alu.add, None, jn)

                def part(r):
                    return R(pn, r * V + v0, r * V + v0 + n)
                tag[0] = "pg%d" % c
                if CFG["ps"][c]:
                    gather(CFG["pg"][c][0], part(rank), win, lk, n)
                    arr = exchange(t + 1, c, part, 256 * n)[1]
                else:
                    arr = exchange(t + 1, c, lambda r: lists(t + 1, r, j0, j0 + jn), 16 * n)[1]
                    for x, r in enumerate(ranks):
                        gather(CFG["pg"][c][x], part(r), win, lists(t + 1, r, j0, j0 + jn), n, pad=0.0 if last or r == rank else CFG["pad"])
                copies(t + 1, c, after=arr if c >= nc - 2 else [])
            if not merge:
                tag[0] = "ahl" if last else "ah%d" % c
                bytes_of_winner()
                to_lists(Q, 1 if last or ride else 2, 4)
            for cs in CFG["reg"][t]:
                if cs[-1] == c:
                    banks = sorted(set(sum([qb[x] for x in cs if x < nc - 1], []))) + [Q] * last
                    new_ends(cs, banks[:2] if len(banks) == 3 else banks[:4])
        if final:
            tag[0] = "out"
            ts(R("ycf", 0, 64), R("c16", 0, 64), 2048.0, None, Alu.add, None, 64)
            dma("S", "d_yc", ("yc", (full, full)), R("ycf", 0, 64)[:2], 32768, [R("ycf", 0, 64)], [])
            dma("S", "d_yx", ("yx", (full, full)), R("yxf", 0, 64)[:2], 32768, [R("yxf", 0, 64)], [])
    return ops


def depend(ops):
    hist, turns, deps, group = {}, {}, [], {}
    for i, o in enumerate(ops):
        d = set()
        acc = [(r, False) for r in o["rd"]] + [(r, True) for r in o["wr"]]
        for r, wr in acc:
            for (k, s, w2) in hist.get(r[0], []):
                if (wr or w2) and meet(r, s):
                    d.add(k)
        for name in sorted(set(r[0] for r, wr in acc if in_psum(r))):
            tn = turns.setdefault(name, [o["eng"], [], []])
            if tn[0] != o["eng"]:
                tn[:] = [o["eng"], [], tn[1]]
            d.update(tn[2])
            if o["eng"] == "P":
                d.update(tn[1][-1:])
            tn[1].append(i)
        for r, wr in acc:
            h = hist.setdefault(r[0], [])
            if wr and len(r[1]) == 2 and r[1][1].step is None:
                h[:] = [e for e in h if not (r[2] <= e[1][2] and e[1][3] <= r[3])]
            elif wr:
                h[:] = [e for e in h if e[1][1] != r[1]]
            h.append((i, r, wr))
        for k in list(d):
            d.update(group.get(ops[k]["sem"], []))
        if o["sem"] is not None:
            group.setdefault(o["sem"], []).append(i)
        deps.append(sorted(d))
    return deps


def times(o, P):
    kind, n = o["cost"][:2]
    if kind == "v":
        c = max(64, n) * P["cyc"] + P["fix"]
    elif kind == "g":
        c = n * P["gam"] * P["cyc"] + (50 if o["eng"] == "V" else 65)
    elif kind == "p":
        c = n * P["pe"]
    elif kind == "i":
        c = 130 + 2 * n * P["cyc"]
    elif kind == "s":
        c = P["issue"] + (P["first"] if n else 0)
    elif kind == "x":
        return 0.0, P["fly"] + 3 * n / P["rbw"]
    elif kind == "gd":
        c = P["gissue"] * (2 if o["cost"][2] else 1)
        return c, c + P["dlat"] + 2 * n / P["dbw"]
    else:
        return 60.0 + (n / P["dbw"] if o["eng"] == "Y" else 0.0), P["dlat"] + n / P["dbw"]
    return c, c


def gap(ops, k, i, P):
    a, b = ops[k]["eng"], ops[i]["eng"]
    if b == "X" or (a == b == "P"):
        return 0.0
    return P["self"] if a == b and ops[k]["sem"] is None else P["lat"]


def sweep(ops, tm, nxt, prio):
    n = len(ops)
    left, ready = [0] * n, [0.0] * n
    for i in range(n):
        for s, lag in nxt[i]:
            left[s] += 1
    cand = {e: [] for e in "VSPGYX"}
    free = {e: 0.0 for e in "VSPGYX"}
    slack = [0.0 if o["tag"] in CFG["urgent"] else CFG["alpha"] for o in ops]
    for i in range(n):
        if not left[i]:
            cand[ops[i]["eng"]].append(i)
    order, picks, stale = [], {}, set(cand)
    while len(order) < n:
        for e in stale:
            pick, limit, f = (math.inf, -1), math.inf, free[e]
            cand[e].sort(key=prio.get)
            for i in cand[e]:
                st = max(ready[i], f)
                if st < pick[0] and st + tm[i][0] <= limit:
                    pick = (st, i)
                if st == f:
                    break
                limit = min(limit, st + 120.0 + slack[i] * (st - f))
            picks[e] = pick
        st, i = min(picks.values())
        e = ops[i]["eng"]
        stale = {e}
        cand[e].remove(i)
        free[e] = st + tm[i][0]
        order.append(i)
        for s, lag in nxt[i]:
            ready[s] = max(ready[s], st + (tm[i][0] if lag is None else tm[i][1] + lag))
            left[s] -= 1
            if not left[s]:
                cand[ops[s]["eng"]].append(s)
                stale.add(ops[s]["eng"])
    return order


def priority(ops, level, pri):
    def place(o):
        key = o["eng"] + o["tag"]
        return pri.get(key + "F", pri.get(key, 90)) if o["round"] == RO - 1 else pri.get(key, 90)
    return {i: (100 * o["round"] + place(o), i) if o["tag"] else (-1000 - level[i], i) for i, o in enumerate(ops)}


def schedule(ops, deps, P):
    n = len(ops)
    succ = [[] for _ in range(n)]
    for i in range(n):
        for k, hard in [(k, True) for k in deps[i]] + [(k, ops[k]["eng"] != ops[i]["eng"]) for k in ops[i]["after"]]:
            succ[k].append((i, gap(ops, k, i, P) + ops[i]["pad"] if hard else None))
    tm = [times(o, P) for o in ops]
    level = [0.0] * n
    for i in range(n - 1, -1, -1):
        level[i] = tm[i][1] + max([level[s] + (lag or 0.0) for s, lag in succ[i]] + [0.0])
    return sweep(ops, tm, succ, priority(ops, level, CFG["pri"]))


def waits(ops, deps, order):
    pos, cnt = {}, {}
    for i in order:
        cnt[ops[i]["eng"]] = cnt.get(ops[i]["eng"], 0) + 1
        pos[i] = cnt[ops[i]["eng"]]
    known = {e: {} for e in "VSPGY"}
    seen, wl = {}, {}
    for i in order:
        e = ops[i]["eng"]
        wl[i] = []
        if e == "X":
            seen[i] = {}
            continue
        kn = known[e]
        need = set(deps[i]) | set(k for k in ops[i]["after"] if ops[k]["eng"] != e)
        for k in sorted(need, key=lambda k: -pos[k]):
            f = ops[k]["eng"]
            if f == e == "P":
                continue
            key = ops[k]["sem"] or ("gi" if ops[k]["call"][0] == "send" else f)
            if kn.get(key, 0) >= pos[k]:
                continue
            wl[i].append(k)
            kn[key] = pos[k]
            for a, v in seen[k].items():
                kn[a] = max(kn.get(a, 0), v)
        seen[i] = dict(kn)
    return wl


def rank_program(g, core, T, topo):
    rank = T.rank_of(core)
    if rank is None:
        return
    ops = build(rank)
    deps = depend(ops)
    order = schedule(ops, deps, NOMINAL)
    wl = waits(ops, deps, order)
    waited = set(k for i in order for k in wl[i])
    queue = {"V": g.vector, "S": g.scalar, "P": g.tensor, "G": g, "Y": g.sync}
    cores = list(T.cores)

    def common(src):
        m = -1
        for d in cores:
            if d != src:
                m &= topo.mask(src, d)
        return m

    def hops(d):
        a, b = topo.chip(core), topo.chip(d)
        return 0 if a == b else 1 if topo.mates(a, b) or topo.same_plane(a, b) else 2
    peers = sorted([d for d in cores if d != core], key=lambda d: -hops(d))
    ids = [DstId(rid=topo.addr(d)[0], pnc=topo.addr(d)[1]) for d in peers]
    mask = common(core)
    width = {r: bin(common(cores[r])).count("1") for r in range(N)}

    def ap(r):
        return T[r[0]][r[1]] if isinstance(r, tuple) else r

    total = {}
    for o in ops:
        total[o["sem"]] = total.get(o["sem"], 0) + 16
    signal, cnt, sends = {}, {}, 0
    for i in order:
        o = ops[i]
        e, c = o["eng"], o["call"]
        if e == "X":
            signal[i] = (o["sem"], width[int(o["sem"][-1])])
            continue
        q = queue[e]
        for k in wl[i]:
            q.wait_ge(T.sem[signal[k][0]], signal[k][1])
        kind = c[0]
        if kind == "send":
            g.remote_dma_fused([RemoteDMATransfer(dst_ids=ids, dma_engine_mask=mask, remote_sem=T.sem[c[2]], srcs=[ap(c[1])],
                                                  dsts=[ap(c[1]) for _ in ids])], local_sem=T.sem["sent"])
            sends += 1
            if i in waited:
                cnt["gi"] = cnt.get("gi", 0) + 1
                g.sem_inc(T.sem["gi"], 1)
                signal[i] = ("gi", cnt["gi"])
            continue
        if kind in ("dma", "gd"):
            if kind == "dma":
                ins = q.dma_start(ap(c[1]), ap(c[2]))
            else:
                ins = q.dma_start(ap(c[1]), ap(c[2]), accum_op=Alu.add, max_dma_last_dim=4096)
            ins.then_inc(T.sem[o["sem"]], 16)
            signal[i] = (o["sem"], total[o["sem"]])
            continue
        if kind == "ts":
            if c[6] is None:
                ins = q.tensor_scalar(ap(c[1]), ap(c[2]), ap(c[3]), None, c[5])
            else:
                ins = q.tensor_scalar(ap(c[1]), ap(c[2]), ap(c[3]), ap(c[4]), c[5], c[6])
        elif kind == "tt":
            ins = q.tensor_tensor(ap(c[1]), ap(c[2]), ap(c[3]), c[4])
        elif kind == "cp":
            ins = q.tensor_copy(ap(c[1]), ap(c[2]))
        elif kind == "ms":
            ins = q.memset(ap(c[1]), c[2])
        elif kind == "act":
            ins = q.activation(ap(c[1]), ap(c[2]), c[3], bias=ap(c[4]), scale=ap(c[5]))
        elif kind == "mm":
            ins = q.matmul(ap(c[1]), ap(c[2]), ap(c[3]), c[4], c[5])
        elif kind == "gv":
            ins = q.tensor_copy(ap(c[1]), ap(c[2]).indirect(ap(c[3])))
        elif kind == "gs":
            ins = q.activation(ap(c[1]), ap(c[2]).indirect(ap(c[3])), Act.Identity, scale=c[4])
        elif kind == "ge":
            ins = q.tensor_tensor(ap(c[1]), ap(c[2]).indirect(ap(c[3])), ap(c[4]), Alu.is_equal)
        elif c[4]:
            ins = q.iota(ap(c[1]), c[2], 0, c[3], allow_small_or_imprecise_dtypes=True)
        else:
            ins = q.iota(ap(c[1]), c[2], 0, c[3])
        if i in waited:
            cnt[e] = cnt.get(e, 0) + 1
            ins.then_inc(T.sem["s" + e], 1)
            signal[i] = ("s" + e, cnt[e])
    g.wait_ge(T.sem["sent"], sends * width[rank])
    done = set(ops[i]["sem"] for i in waited)
    for i in order:
        if ops[i]["sem"] is not None and ops[i]["sem"] not in done:
            done.add(ops[i]["sem"])
            g.sync.wait_ge(T.sem[signal[i][0]], signal[i][1])
